import numpy as np
import ml_dtypes


def mxq(x, axis, fmt="e4m3"):
    dtype, down = {"e4m3": (ml_dtypes.float8_e4m3fn, 7), "e5m2": (ml_dtypes.float8_e5m2, 14)}[fmt]
    v = np.moveaxis(np.asarray(x, np.float32).astype(ml_dtypes.bfloat16).astype(np.float64), axis, -1)
    blocks = v.reshape(v.shape[:-1] + (-1, 32))
    amax = np.abs(blocks).max(-1, keepdims=True)
    byte = np.maximum(np.where(amax > 0, np.frexp(amax)[1] - 1 + 127, 0) - down, 1)
    scale = np.exp2(byte - 127.0)
    codes = (blocks / scale).astype(np.float32).astype(dtype).astype(np.float64)
    return np.moveaxis((codes * scale).reshape(v.shape), -1, axis)


WIDE = False


def mx_kscale(k):
    if not WIDE:
        return np.ones(k)
    levels = np.array([18, -18])
    if k % 512:
        return np.exp2(np.random.permutation(np.resize(levels, k // 32))).repeat(32)
    a = np.empty((k // 512, 16))
    for p in range(k // 512):
        a[p, :8] = np.random.permutation(np.resize(levels, 8))
        for g in range(8):
            far = levels[np.abs(levels - a[p, g]) >= 10]
            a[p, g + 8] = far[np.random.randint(len(far))]
    return np.exp2(a.ravel()).repeat(32)


def f64(x):
    return np.asarray(x).astype(np.float64)


def striped(idx):
    return np.tile(np.asarray(idx).reshape(-1, 16).T, (8, 1)).astype(np.uint16)


def unstriped(offs):
    return offs[:16].T.reshape(-1).astype(np.int64)


B, N, T, D, DV, NQ = 1, 512, 1024, 128, 512, 512


def setup_inputs():
    n = np.random.standard_normal
    idx = np.random.permutation(T)[:B * N]
    s = mx_kscale(DV)[:, None]
    z = mx_kscale(NQ)[:, None]
    p = np.exp(n((B, NQ, N)))
    p = p / p.mean(2, keepdims=True)
    return {
        "doT": (n((B, DV, NQ)) * s / np.sqrt(DV)).astype(np.float32),
        "vT": (n((DV, T)) / s).astype(np.float32),
        "p": (p * z / np.sqrt(NQ)).astype(np.float32),
        "delta": (0.3 * n((B, NQ, 1))).astype(np.float32),
        "qm": (n((B, NQ, D)) / z).astype(np.float32),
        "offs": striped(idx),
    }


def reference(doT, vT, p, delta, qm, offs):
    idx = unstriped(offs)
    pick = lambda x: x[:, idx].reshape(x.shape[0], B, N).transpose(1, 0, 2)
    dp = mxq(f64(doT), 1, "e5m2").transpose(0, 2, 1) @ mxq(pick(f64(vT)), 1, "e4m3")
    ds = f64(p) * (dp - f64(delta))
    dk = mxq(f64(qm), 1, "e4m3").transpose(0, 2, 1) @ mxq(ds, 1, "e5m2")
    out = np.zeros((D, T))
    out[:, idx] = dk.transpose(1, 0, 2).reshape(D, B * N)
    return out

@@ -1,0 +1,229 @@
+from contextlib import ExitStack
+
+import concourse.mybir as mybir
+from concourse.masks import make_identity
+
+FLOPS = 335544320
+
+F32 = mybir.dt.float32
+BF16 = mybir.dt.bfloat16
+U32 = mybir.dt.uint32
+U16 = mybir.dt.uint16
+U8 = mybir.dt.uint8
+E4M3X4 = mybir.dt.float8_e4m3fn_x4
+E5M2X4 = mybir.dt.float8_e5m2_x4
+ACT = mybir.ActivationFunctionType
+ALU = mybir.AluOpType
+
+P = 128
+J = 4
+E = 512
+Q = 512
+N = 512
+T = 1024
+D = 128
+H = 2
+NH = N // H
+NA = 128
+NV = 320
+QH = Q // 2
+
+
+def tile_attend_bwd_kernel(tc, doT, vT, p, delta, qm, offs, out):
+    nc = tc.nc
+    with ExitStack() as ctx:
+        keep = ctx.enter_context(tc.tile_pool(name="keep", bufs=1))
+        psum = ctx.enter_context(tc.psum_pool(name="psum", bufs=1))
+
+        offsets = keep.tile([P, N // 16], U16, name="offsets")
+
+        v_rows = vT.rearrange("(p j) t -> p j t", j=J)
+        v_raw = []
+        for j in range(J):
+            t = keep.tile([P, T], F32, name=f"v_raw{j}")
+            nc.sync.dma_start(out=t[:], in_=v_rows[:, j, :])
+            v_raw.append(t)
+            if j == 0:
+                nc.sync.dma_start(offsets[:], offs)
+
+        do_rows = doT[0].rearrange("(p j) q -> p j q", j=J)
+        do_raw = []
+        for h in range(2):
+            t = keep.tile([P, J, QH], F32, name=f"do_raw{h}")
+            nc.sync.dma_start(out=t[:], in_=do_rows[:, :, h * QH : (h + 1) * QH])
+            do_raw.append(t)
+
+        p_rows = p[0].rearrange("(p j) s -> p j s", j=J)
+        p_raw = {}
+        for h in (1, 0):
+            t = keep.tile([P, J, NH], F32, name=f"p_raw{h}")
+            nc.sync.dma_start(out=t[:], in_=p_rows[:, :, h * NH : (h + 1) * NH])
+            p_raw[h] = t
+            if h == 1:
+                qm_raw = keep.tile([P, J, D], F32, name="qm_raw")
+                nc.sync.dma_start(out=qm_raw[:], in_=qm[0].rearrange("(p j) d -> p j d", j=J))
+
+        delta_col = keep.tile([P, J], F32, name="delta_col")
+        nc.scalar.dma_start(out=delta_col[:], in_=delta[0].rearrange("(p j) o -> p (j o)", j=J))
+        minus_delta = keep.tile([P, J], F32, name="minus_delta")
+        nc.gpsimd.tensor_scalar(minus_delta[:], delta_col[:], -1.0, None, ALU.mult)
+
+        warm = keep.tile([P, 1], F32, name="warm")
+        warm_out = keep.tile([P, 1], F32, name="warm_out")
+        nc.gpsimd.memset(warm[:], 0.0)
+        nc.scalar.activation(warm_out[:], warm[:], ACT.Identity)
+        window = keep.tile([P, T], F32, name="window")
+        nc.gpsimd.memset(window[:], 0.0)
+        ds_codes = []
+        ds_scales = []
+        for h in range(2):
+            c = keep.tile([P, N], U32, name=f"ds_codes{h}", align_bytes=64)
+            s = keep.tile([P, N], U8, name=f"ds_scales{h}", align_bytes=64)
+            fill = slice(NA, N) if h == 0 else slice(0, NA)
+            nc.gpsimd.memset(c[:, fill], 0)
+            nc.gpsimd.memset(s[:, fill].bitcast(U32), 0)
+            ds_codes.append(c)
+            ds_scales.append(s)
+
+        identity = keep.tile([P, P], F32, name="identity")
+        make_identity(nc, identity[:])
+        spare = []
+        for b in range(2):
+            spare.append(psum.tile([P, 4, P], F32, name=f"spare{b}"))
+        turns = [0]
+
+        def keep_warm(src):
+            b = turns[0] % 8
+            turns[0] += 1
+            nc.tensor.transpose(spare[b // 4][:, b % 4, :], src, identity[:])
+
+        v_got = keep.tile([P, J, N], F32, name="v_got")
+        v_cols = keep.tile([P, J * N], BF16, name="v_cols", align_bytes=64)
+
+        def interleave_v(engine_copy, pair, s0, s1):
+            js = slice(2 * pair, 2 * pair + 2)
+            engine_copy(
+                v_cols[:, J * s0 : J * s1].rearrange("p (c i j) -> p c j i", i=4, j=J)[:, :, js, :],
+                v_got[:, js, s0:s1].rearrange("p j (c i) -> p c j i", i=4),
+            )
+
+        for j in range(J):
+            nc.vector.tensor_copy(v_got[:, j, :], v_raw[j][:].indirect(offsets[:]))
+            if j == 1:
+                interleave_v(nc.scalar.copy, 0, 0, N)
+        for b in range(10):
+            keep_warm(v_raw[3][:, b % 8 * P : (b % 8 + 1) * P])
+        for h, n in ((0, 8), (1, 6)):
+            for b in range(n):
+                keep_warm(do_raw[h][:, b // 2, b % 2 * P : (b % 2 + 1) * P])
+        interleave_v(nc.vector.tensor_copy, 1, 0, NV)
+        interleave_v(nc.scalar.copy, 1, NV, N)
+
+        do_cols = keep.tile([P, J * Q], BF16, name="do_cols", align_bytes=64)
+        do_view = do_cols[:].rearrange("p (t m j) -> p m j t", t=J, j=J)
+        MH = QH // J
+        v_codes = keep.tile([P, N], U32, name="v_codes", align_bytes=64)
+        v_scales = keep.tile([P, N], U8, name="v_scales", align_bytes=64)
+        nc.vector.quantize_mx(out=v_codes[:].bitcast(E4M3X4), scales=v_scales[:], in_=v_cols[:])
+        for h, m0, m1 in ((0, 0, MH), (1, 0, MH // 2), (1, MH // 2, MH)):
+            dst = do_view[:, h * MH + m0 : h * MH + m1, :, :]
+            src = do_raw[h][:, :, m0 * J : m1 * J].rearrange("p j (m t) -> p m j t", t=J)
+            if m0 == 0:
+                nc.scalar.activation(dst, src, ACT.Copy)
+            else:
+                nc.vector.tensor_copy(dst, src)
+
+        do_codes = keep.tile([P, Q], U32, name="do_codes", align_bytes=64)
+        do_scales = keep.tile([P, Q], U8, name="do_scales", align_bytes=64)
+        dp = []
+        for t in range(J):
+            cols = slice(t * P, (t + 1) * P)
+            nc.vector.quantize_mx(
+                out=do_codes[:, cols].bitcast(E5M2X4),
+                scales=do_scales[:, cols],
+                in_=do_cols[:, t * P * J : (t + 1) * P * J],
+            )
+            bank = psum.tile([P, N], F32, name=f"dp{t}")
+            nc.tensor.matmul_mx(
+                out=bank[:],
+                lhsT=do_codes[:, cols].bitcast(E5M2X4),
+                lhsT_scale=do_scales[:, cols],
+                rhs=v_codes[:].bitcast(E4M3X4),
+                rhs_scale=v_scales[:],
+                start=True,
+                stop=True,
+            )
+            dp.append(bank)
+
+        qm_cols = keep.tile([P, J * D], BF16, name="qm_cols", align_bytes=64)
+        nc.gpsimd.tensor_scalar(
+            qm_cols[:].rearrange("p (c i j) -> p c j i", i=4, j=J),
+            qm_raw[:].rearrange("p j (c i) -> p c j i", i=4),
+            1.0,
+            0.0,
+            ALU.mult,
+            ALU.add,
+        )
+        qm_codes = keep.tile([P, D], U32, name="qm_codes", align_bytes=64)
+        qm_scales = keep.tile([P, D], U8, name="qm_scales", align_bytes=64)
+
+        x = keep.tile([P, J, NH], F32, name="x")
+        ds_rows = keep.tile([P, J, NH], BF16, name="ds_rows")
+        for t in range(J):
+            nc.scalar.activation(x[:, t, :], dp[t][:, 0:NH], ACT.Identity, bias=minus_delta[:, t : t + 1])
+            nc.vector.scalar_tensor_tensor(
+                ds_rows[:, t, :], dp[t][:, NH:N], delta_col[:, t : t + 1], p_raw[1][:, t, :], ALU.subtract, ALU.mult
+            )
+        for t in range(J):
+            for b in range(NH // P):
+                keep_warm(x[:, t, b * P : (b + 1) * P])
+        for t in range(J):
+            for b in range(NH // P):
+                keep_warm(p_raw[0][:, t, b * P : (b + 1) * P])
+        ds_tail = keep.tile([P, J * NH], BF16, name="ds_tail", align_bytes=64)
+        nc.scalar.copy(
+            ds_tail[:].rearrange("p (c i j) -> p c j i", i=4, j=J),
+            ds_rows[:].rearrange("p j (c i) -> p c j i", i=4),
+        )
+        nc.vector.quantize_mx(out=qm_codes[:].bitcast(E4M3X4), scales=qm_scales[:], in_=qm_cols[:])
+        ds_head = []
+        for a in range(2):
+            cols = slice(a * NA, (a + 1) * NA)
+            d = keep.tile([P, J * NA], BF16, name=f"ds_head{a}", align_bytes=64)
+            nc.vector.tensor_tensor(
+                d[:].rearrange("p (c i j) -> p c j i", i=4, j=J),
+                x[:, :, cols].rearrange("p j (c i) -> p c j i", i=4),
+                p_raw[0][:, :, cols].rearrange("p j (c i) -> p c j i", i=4),
+                ALU.mult,
+            )
+            ds_head.append(d)
+
+        def quantise_ds(h, cols, src):
+            nc.vector.quantize_mx(out=ds_codes[h][:, cols].bitcast(E5M2X4), scales=ds_scales[h][:, cols], in_=src)
+
+        dk_cols = []
+
+        def keys_gradient(h, cols):
+            dk = psum.tile([P, N], F32, name=f"dk{h}")
+            nc.tensor.matmul_mx(
+                out=dk[:],
+                lhsT=qm_codes[:].bitcast(E4M3X4),
+                lhsT_scale=qm_scales[:],
+                rhs=ds_codes[h][:].bitcast(E5M2X4),
+                rhs_scale=ds_scales[h][:],
+                start=True,
+                stop=True,
+            )
+            for c0, c1 in cols:
+                d = keep.tile([P, c1 - c0], F32, name=f"dk_cols{c0}")
+                nc.scalar.activation(d[:], dk[:, c0:c1], ACT.Copy)
+                dk_cols.append((c0, c1, d))
+
+        quantise_ds(0, slice(0, NA), ds_head[0][:])
+        keys_gradient(0, ((0, NA),))
+        quantise_ds(1, slice(NA, NH), ds_head[1][:])
+        quantise_ds(1, slice(NH, N), ds_tail[:])
+        keys_gradient(1, ((NA, N),))
+        for c0, c1, d in dk_cols:
+            nc.vector.tensor_copy(window[:].indirect(offsets[:, c0 // 16 : c1 // 16]), d[:])
+        nc.sync.dma_start(out=out, in_=window[:])

@@ -1,7 +1,6 @@
 from contextlib import ExitStack
 
 import concourse.mybir as mybir
-from concourse.masks import make_identity
 
 FLOPS = 335544320
 
@@ -12,7 +11,6 @@ U16 = mybir.dt.uint16
 U8 = mybir.dt.uint8
 E4M3X4 = mybir.dt.float8_e4m3fn_x4
 E5M2X4 = mybir.dt.float8_e5m2_x4
-ACT = mybir.ActivationFunctionType
 ALU = mybir.AluOpType
 
 P = 128
@@ -22,11 +20,11 @@ Q = 512
 N = 512
 T = 1024
 D = 128
-H = 2
-NH = N // H
 NA = 128
-NV = 320
+NV = 384
 QH = Q // 2
+WEAVE_OUT = "p (c i j) -> p c j i"
+WEAVE_IN = "p j (c i) -> p c j i"
 
 
 def tile_attend_bwd_kernel(tc, doT, vT, p, delta, qm, offs, out):
@@ -53,96 +51,74 @@ def tile_attend_bwd_kernel(tc, doT, vT, p, delta, qm, offs, out):
             nc.sync.dma_start(out=t[:], in_=do_rows[:, :, h * QH : (h + 1) * QH])
             do_raw.append(t)
 
+        qm_raw = keep.tile([P, J, D], F32, name="qm_raw")
+        nc.sync.dma_start(out=qm_raw[:], in_=qm[0].rearrange("(p j) d -> p j d", j=J))
+
         p_rows = p[0].rearrange("(p j) s -> p j s", j=J)
-        p_raw = {}
-        for h in (1, 0):
-            t = keep.tile([P, J, NH], F32, name=f"p_raw{h}")
-            nc.sync.dma_start(out=t[:], in_=p_rows[:, :, h * NH : (h + 1) * NH])
-            p_raw[h] = t
-            if h == 1:
-                qm_raw = keep.tile([P, J, D], F32, name="qm_raw")
-                nc.sync.dma_start(out=qm_raw[:], in_=qm[0].rearrange("(p j) d -> p j d", j=J))
+        p_raw = []
+        for h in range(2):
+            t = keep.tile([P, 2, N], F32, name=f"p_raw{h}")
+            nc.sync.dma_start(out=t[:], in_=p_rows[:, 2 * h : 2 * h + 2, :])
+            p_raw.append(t)
 
         delta_col = keep.tile([P, J], F32, name="delta_col")
         nc.scalar.dma_start(out=delta_col[:], in_=delta[0].rearrange("(p j) o -> p (j o)", j=J))
-        minus_delta = keep.tile([P, J], F32, name="minus_delta")
-        nc.gpsimd.tensor_scalar(minus_delta[:], delta_col[:], -1.0, None, ALU.mult)
 
-        warm = keep.tile([P, 1], F32, name="warm")
-        warm_out = keep.tile([P, 1], F32, name="warm_out")
-        nc.gpsimd.memset(warm[:], 0.0)
-        nc.scalar.activation(warm_out[:], warm[:], ACT.Identity)
         window = keep.tile([P, T], F32, name="window")
         nc.gpsimd.memset(window[:], 0.0)
-        ds_codes = []
-        ds_scales = []
-        for h in range(2):
-            c = keep.tile([P, N], U32, name=f"ds_codes{h}", align_bytes=64)
-            s = keep.tile([P, N], U8, name=f"ds_scales{h}", align_bytes=64)
-            fill = slice(NA, N) if h == 0 else slice(0, NA)
-            nc.gpsimd.memset(c[:, fill], 0)
-            nc.gpsimd.memset(s[:, fill].bitcast(U32), 0)
-            ds_codes.append(c)
-            ds_scales.append(s)
+        FILL = N - NA
+        ds_codes = keep.tile([P, FILL + N], U32, name="ds_codes", align_bytes=64)
+        ds_scales = keep.tile([P, FILL + N], U8, name="ds_scales", align_bytes=64)
+        nc.gpsimd.memset(ds_codes[:, 0:FILL], 0)
+        nc.gpsimd.memset(ds_scales[:, 0:FILL].bitcast(U32), 0)
 
-        identity = keep.tile([P, P], F32, name="identity")
-        make_identity(nc, identity[:])
-        spare = []
-        for b in range(2):
-            spare.append(psum.tile([P, 4, P], F32, name=f"spare{b}"))
-        turns = [0]
-
-        def keep_warm(src):
-            b = turns[0] % 8
-            turns[0] += 1
-            nc.tensor.transpose(spare[b // 4][:, b % 4, :], src, identity[:])
+        def weave_pair(engine_copy, dst, src, pair):
+            js = slice(2 * pair, 2 * pair + 2)
+            engine_copy(
+                dst.rearrange(WEAVE_OUT, i=4, j=J)[:, :, js, :],
+                src[:, js, :].rearrange(WEAVE_IN, i=4),
+            )
 
         v_got = keep.tile([P, J, N], F32, name="v_got")
         v_cols = keep.tile([P, J * N], BF16, name="v_cols", align_bytes=64)
-
-        def interleave_v(engine_copy, pair, s0, s1):
-            js = slice(2 * pair, 2 * pair + 2)
-            engine_copy(
-                v_cols[:, J * s0 : J * s1].rearrange("p (c i j) -> p c j i", i=4, j=J)[:, :, js, :],
-                v_got[:, js, s0:s1].rearrange("p j (c i) -> p c j i", i=4),
-            )
-
         for j in range(J):
             nc.vector.tensor_copy(v_got[:, j, :], v_raw[j][:].indirect(offsets[:]))
             if j == 1:
-                interleave_v(nc.scalar.copy, 0, 0, N)
-        for b in range(10):
-            keep_warm(v_raw[3][:, b % 8 * P : (b % 8 + 1) * P])
-        for h, n in ((0, 8), (1, 6)):
-            for b in range(n):
-                keep_warm(do_raw[h][:, b // 2, b % 2 * P : (b % 2 + 1) * P])
-        interleave_v(nc.vector.tensor_copy, 1, 0, NV)
-        interleave_v(nc.scalar.copy, 1, NV, N)
+                weave_pair(nc.scalar.copy, v_cols[:], v_got[:], 0)
 
         do_cols = keep.tile([P, J * Q], BF16, name="do_cols", align_bytes=64)
         do_view = do_cols[:].rearrange("p (t m j) -> p m j t", t=J, j=J)
         MH = QH // J
+        MV = 44
+        M0 = 24
+
+        def weave_do(engine_copy, h, m0, m1):
+            engine_copy(
+                do_view[:, h * MH + m0 : h * MH + m1, :, :],
+                do_raw[h][:, :, m0 * J : m1 * J].rearrange("p j (m t) -> p m j t", t=J),
+            )
+
+        weave_do(nc.scalar.copy, 0, 0, M0)
+        weave_pair(nc.vector.tensor_copy, v_cols[:, 0 : J * NV], v_got[:, :, 0:NV], 1)
+        weave_pair(nc.scalar.copy, v_cols[:, J * NV : J * N], v_got[:, :, NV:N], 1)
         v_codes = keep.tile([P, N], U32, name="v_codes", align_bytes=64)
         v_scales = keep.tile([P, N], U8, name="v_scales", align_bytes=64)
         nc.vector.quantize_mx(out=v_codes[:].bitcast(E4M3X4), scales=v_scales[:], in_=v_cols[:])
-        for h, m0, m1 in ((0, 0, MH), (1, 0, MH // 2), (1, MH // 2, MH)):
-            dst = do_view[:, h * MH + m0 : h * MH + m1, :, :]
-            src = do_raw[h][:, :, m0 * J : m1 * J].rearrange("p j (m t) -> p m j t", t=J)
-            if m0 == 0:
-                nc.scalar.activation(dst, src, ACT.Copy)
-            else:
-                nc.vector.tensor_copy(dst, src)
+        weave_do(nc.scalar.copy, 0, M0, MH)
+        weave_do(nc.scalar.copy, 1, 0, MH - MV)
+        weave_do(nc.vector.tensor_copy, 1, MH - MV, MH)
 
         do_codes = keep.tile([P, Q], U32, name="do_codes", align_bytes=64)
         do_scales = keep.tile([P, Q], U8, name="do_scales", align_bytes=64)
+        for t0, t1 in ((0, 1), (1, 2), (2, 4)):
+            nc.vector.quantize_mx(
+                out=do_codes[:, t0 * P : t1 * P].bitcast(E5M2X4),
+                scales=do_scales[:, t0 * P : t1 * P],
+                in_=do_cols[:, t0 * P * J : t1 * P * J],
+            )
         dp = []
         for t in range(J):
             cols = slice(t * P, (t + 1) * P)
-            nc.vector.quantize_mx(
-                out=do_codes[:, cols].bitcast(E5M2X4),
-                scales=do_scales[:, cols],
-                in_=do_cols[:, t * P * J : (t + 1) * P * J],
-            )
             bank = psum.tile([P, N], F32, name=f"dp{t}")
             nc.tensor.matmul_mx(
                 out=bank[:],
@@ -156,74 +132,66 @@ def tile_attend_bwd_kernel(tc, doT, vT, p, delta, qm, offs, out):
             dp.append(bank)
 
         qm_cols = keep.tile([P, J * D], BF16, name="qm_cols", align_bytes=64)
-        nc.gpsimd.tensor_scalar(
-            qm_cols[:].rearrange("p (c i j) -> p c j i", i=4, j=J),
-            qm_raw[:].rearrange("p j (c i) -> p c j i", i=4),
-            1.0,
-            0.0,
-            ALU.mult,
-            ALU.add,
-        )
+        nc.scalar.copy(qm_cols[:].rearrange(WEAVE_OUT, i=4, j=J), qm_raw[:].rearrange(WEAVE_IN, i=4))
         qm_codes = keep.tile([P, D], U32, name="qm_codes", align_bytes=64)
         qm_scales = keep.tile([P, D], U8, name="qm_scales", align_bytes=64)
-
-        x = keep.tile([P, J, NH], F32, name="x")
-        ds_rows = keep.tile([P, J, NH], BF16, name="ds_rows")
-        for t in range(J):
-            nc.scalar.activation(x[:, t, :], dp[t][:, 0:NH], ACT.Identity, bias=minus_delta[:, t : t + 1])
-            nc.vector.scalar_tensor_tensor(
-                ds_rows[:, t, :], dp[t][:, NH:N], delta_col[:, t : t + 1], p_raw[1][:, t, :], ALU.subtract, ALU.mult
-            )
-        for t in range(J):
-            for b in range(NH // P):
-                keep_warm(x[:, t, b * P : (b + 1) * P])
-        for t in range(J):
-            for b in range(NH // P):
-                keep_warm(p_raw[0][:, t, b * P : (b + 1) * P])
-        ds_tail = keep.tile([P, J * NH], BF16, name="ds_tail", align_bytes=64)
-        nc.scalar.copy(
-            ds_tail[:].rearrange("p (c i j) -> p c j i", i=4, j=J),
-            ds_rows[:].rearrange("p j (c i) -> p c j i", i=4),
-        )
         nc.vector.quantize_mx(out=qm_codes[:].bitcast(E4M3X4), scales=qm_scales[:], in_=qm_cols[:])
-        ds_head = []
-        for a in range(2):
-            cols = slice(a * NA, (a + 1) * NA)
-            d = keep.tile([P, J * NA], BF16, name=f"ds_head{a}", align_bytes=64)
-            nc.vector.tensor_tensor(
-                d[:].rearrange("p (c i j) -> p c j i", i=4, j=J),
-                x[:, :, cols].rearrange("p j (c i) -> p c j i", i=4),
-                p_raw[0][:, :, cols].rearrange("p j (c i) -> p c j i", i=4),
+
+        ds_rows = keep.tile([P, J, N], BF16, name="ds_rows")
+
+        def weigh(t, s0, s1):
+            nc.vector.scalar_tensor_tensor(
+                ds_rows[:, t, s0:s1],
+                dp[t][:, s0:s1],
+                delta_col[:, t : t + 1],
+                p_raw[t // 2][:, t % 2, s0:s1],
+                ALU.subtract,
                 ALU.mult,
             )
-            ds_head.append(d)
 
-        def quantise_ds(h, cols, src):
-            nc.vector.quantize_mx(out=ds_codes[h][:, cols].bitcast(E5M2X4), scales=ds_scales[h][:, cols], in_=src)
+        NH = N // 2
+        ds_low = keep.tile([P, J * NH], BF16, name="ds_low", align_bytes=64)
+        ds_high = keep.tile([P, J * NH], BF16, name="ds_high", align_bytes=64)
+
+        def pool_copy(dst, src):
+            nc.gpsimd.tensor_scalar(dst, src, 1.0, 0.0, ALU.mult, ALU.add)
+
+        def quantise_ds(s0, s1, src):
+            cols = slice(FILL + s0, FILL + s1)
+            nc.vector.quantize_mx(out=ds_codes[:, cols].bitcast(E5M2X4), scales=ds_scales[:, cols], in_=src)
 
         dk_cols = []
 
-        def keys_gradient(h, cols):
+        def keys_gradient(h, first, c0, c1):
             dk = psum.tile([P, N], F32, name=f"dk{h}")
             nc.tensor.matmul_mx(
                 out=dk[:],
                 lhsT=qm_codes[:].bitcast(E4M3X4),
                 lhsT_scale=qm_scales[:],
-                rhs=ds_codes[h][:].bitcast(E5M2X4),
-                rhs_scale=ds_scales[h][:],
+                rhs=ds_codes[:, first : first + N].bitcast(E5M2X4),
+                rhs_scale=ds_scales[:, first : first + N],
                 start=True,
                 stop=True,
             )
-            for c0, c1 in cols:
-                d = keep.tile([P, c1 - c0], F32, name=f"dk_cols{c0}")
-                nc.scalar.activation(d[:], dk[:, c0:c1], ACT.Copy)
-                dk_cols.append((c0, c1, d))
+            d = keep.tile([P, c1 - c0], F32, name=f"dk_cols{c0}")
+            nc.scalar.copy(d[:], dk[:, FILL - first + c0 : FILL - first + c1])
+            dk_cols.append((c0, c1, d))
 
-        quantise_ds(0, slice(0, NA), ds_head[0][:])
-        keys_gradient(0, ((0, NA),))
-        quantise_ds(1, slice(NA, NH), ds_head[1][:])
-        quantise_ds(1, slice(NH, N), ds_tail[:])
-        keys_gradient(1, ((NA, N),))
+        weigh(0, 0, N)
+        weigh(1, 0, N)
+        weave_pair(nc.scalar.copy, ds_low[:], ds_rows[:, :, 0:NH], 0)
+        weave_pair(pool_copy, ds_high[:], ds_rows[:, :, NH:N], 0)
+        weigh(2, 0, N)
+        weigh(3, 0, NA)
+        weigh(3, NA, N)
+        weave_pair(nc.scalar.copy, ds_high[:], ds_rows[:, :, NH:N], 1)
+        weave_pair(nc.vector.tensor_copy, ds_low[:, 0 : J * NA], ds_rows[:, :, 0:NA], 1)
+        weave_pair(nc.vector.tensor_copy, ds_low[:, J * NA : J * NH], ds_rows[:, :, NA:NH], 1)
+        quantise_ds(0, NA, ds_low[:, 0 : J * NA])
+        keys_gradient(0, 0, 0, NA)
+        quantise_ds(NA, NH, ds_low[:, J * NA : J * NH])
+        quantise_ds(NH, N, ds_high[:])
+        keys_gradient(1, FILL, NA, N)
         for c0, c1, d in dk_cols:
             nc.vector.tensor_copy(window[:].indirect(offsets[:, c0 // 16 : c1 // 16]), d[:])
         nc.sync.dma_start(out=out, in_=window[:])

@@ -12,6 +12,7 @@ U8 = mybir.dt.uint8
 E4M3X4 = mybir.dt.float8_e4m3fn_x4
 E5M2X4 = mybir.dt.float8_e5m2_x4
 ALU = mybir.AluOpType
+ACT = mybir.ActivationFunctionType
 
 P = 128
 J = 4
@@ -45,11 +46,9 @@ def tile_attend_bwd_kernel(tc, doT, vT, p, delta, qm, offs, out):
                 nc.sync.dma_start(offsets[:], offs)
 
         do_rows = doT[0].rearrange("(p j) q -> p j q", j=J)
-        do_raw = []
+        do_raw = keep.tile([P, 2, J, QH], F32, name="do_raw")
         for h in range(2):
-            t = keep.tile([P, J, QH], F32, name=f"do_raw{h}")
-            nc.sync.dma_start(out=t[:], in_=do_rows[:, :, h * QH : (h + 1) * QH])
-            do_raw.append(t)
+            nc.sync.dma_start(out=do_raw[:, h, :, :], in_=do_rows[:, :, h * QH : (h + 1) * QH])
 
         qm_raw = keep.tile([P, J, D], F32, name="qm_raw")
         nc.sync.dma_start(out=qm_raw[:], in_=qm[0].rearrange("(p j) d -> p j d", j=J))
@@ -79,42 +78,49 @@ def tile_attend_bwd_kernel(tc, doT, vT, p, delta, qm, offs, out):
                 src[:, js, :].rearrange(WEAVE_IN, i=4),
             )
 
-        v_got = keep.tile([P, J, N], F32, name="v_got")
         v_cols = keep.tile([P, J * N], BF16, name="v_cols", align_bytes=64)
-        for j in range(J):
+        v_lanes = v_cols[:].rearrange("p (s j) -> p s j", j=J)
+        v_cast = keep.tile([P, T], BF16, name="v_cast")
+        v_got = keep.tile([P, J, N], F32, name="v_got")
+        nc.vector.tensor_copy(v_lanes[:, :, 0], v_raw[0][:].indirect(offsets[:]))
+        nc.vector.tensor_copy(v_cast[:], v_raw[1][:])
+        nc.scalar.activation(v_lanes[:, :, 1], v_cast[:].indirect(offsets[:]), ACT.Copy)
+        for j in (2, 3):
             nc.vector.tensor_copy(v_got[:, j, :], v_raw[j][:].indirect(offsets[:]))
-            if j == 1:
-                weave_pair(nc.scalar.copy, v_cols[:], v_got[:], 0)
 
-        do_cols = keep.tile([P, J * Q], BF16, name="do_cols", align_bytes=64)
-        do_view = do_cols[:].rearrange("p (t m j) -> p m j t", t=J, j=J)
+        do_cols = [keep.tile([P, 2 * J * P], BF16, name=f"do_cols{pair}", align_bytes=64) for pair in range(2)]
+
         MH = QH // J
-        MV = 44
-        M0 = 24
+        MV = 16
 
-        def weave_do(engine_copy, h, m0, m1):
+        def weave_do(engine_copy, hs, ms, pair):
             engine_copy(
-                do_view[:, h * MH + m0 : h * MH + m1, :, :],
-                do_raw[h][:, :, m0 * J : m1 * J].rearrange("p j (m t) -> p m j t", t=J),
+                do_cols[pair][:].rearrange("p (t h m j) -> p h m j t", t=2, h=2, j=J)[:, hs, ms, :, :],
+                do_raw[:].rearrange("p h j (m t) -> p h m j t", t=J)[:, hs, ms, :, 2 * pair : 2 * pair + 2],
             )
 
-        weave_do(nc.scalar.copy, 0, 0, M0)
+        weave_do(nc.scalar.copy, slice(0, 1), slice(0, MH), 0)
         weave_pair(nc.vector.tensor_copy, v_cols[:, 0 : J * NV], v_got[:, :, 0:NV], 1)
         weave_pair(nc.scalar.copy, v_cols[:, J * NV : J * N], v_got[:, :, NV:N], 1)
+        weave_do(nc.vector.tensor_copy, slice(0, 2), slice(MH - MV, MH), 1)
         v_codes = keep.tile([P, N], U32, name="v_codes", align_bytes=64)
         v_scales = keep.tile([P, N], U8, name="v_scales", align_bytes=64)
         nc.vector.quantize_mx(out=v_codes[:].bitcast(E4M3X4), scales=v_scales[:], in_=v_cols[:])
-        weave_do(nc.scalar.copy, 0, M0, MH)
-        weave_do(nc.scalar.copy, 1, 0, MH - MV)
-        weave_do(nc.vector.tensor_copy, 1, MH - MV, MH)
+        weave_do(nc.scalar.copy, slice(1, 2), slice(0, MH), 0)
+        weave_do(nc.scalar.copy, slice(0, 2), slice(0, MH - MV), 1)
 
         do_codes = keep.tile([P, Q], U32, name="do_codes", align_bytes=64)
         do_scales = keep.tile([P, Q], U8, name="do_scales", align_bytes=64)
+        qm_cols = do_cols[0][:, 0 : J * D]
+        qm_codes = keep.tile([P, D], U32, name="qm_codes", align_bytes=64)
+        qm_scales = keep.tile([P, D], U8, name="qm_scales", align_bytes=64)
         for t0, t1 in ((0, 1), (1, 2), (2, 4)):
+            if t0 == 2:
+                nc.vector.tensor_copy(qm_cols.rearrange(WEAVE_OUT, i=4, j=J), qm_raw[:].rearrange(WEAVE_IN, i=4))
             nc.vector.quantize_mx(
                 out=do_codes[:, t0 * P : t1 * P].bitcast(E5M2X4),
                 scales=do_scales[:, t0 * P : t1 * P],
-                in_=do_cols[:, t0 * P * J : t1 * P * J],
+                in_=do_cols[t0 // 2][:, t0 % 2 * P * J : (t0 % 2 + t1 - t0) * P * J],
             )
         dp = []
         for t in range(J):
@@ -131,11 +137,7 @@ def tile_attend_bwd_kernel(tc, doT, vT, p, delta, qm, offs, out):
             )
             dp.append(bank)
 
-        qm_cols = keep.tile([P, J * D], BF16, name="qm_cols", align_bytes=64)
-        nc.scalar.copy(qm_cols[:].rearrange(WEAVE_OUT, i=4, j=J), qm_raw[:].rearrange(WEAVE_IN, i=4))
-        qm_codes = keep.tile([P, D], U32, name="qm_codes", align_bytes=64)
-        qm_scales = keep.tile([P, D], U8, name="qm_scales", align_bytes=64)
-        nc.vector.quantize_mx(out=qm_codes[:].bitcast(E4M3X4), scales=qm_scales[:], in_=qm_cols[:])
+        nc.vector.quantize_mx(out=qm_codes[:].bitcast(E4M3X4), scales=qm_scales[:], in_=qm_cols)
 
         ds_rows = keep.tile([P, J, N], BF16, name="ds_rows")
 
@@ -150,8 +152,12 @@ def tile_attend_bwd_kernel(tc, doT, vT, p, delta, qm, offs, out):
             )
 
         NH = N // 2
-        ds_low = keep.tile([P, J * NH], BF16, name="ds_low", align_bytes=64)
-        ds_high = keep.tile([P, J * NH], BF16, name="ds_high", align_bytes=64)
+        NW = 320
+        ds_low = keep.tile([P, J * NA], BF16, name="ds_low", align_bytes=64)
+        ds_high = keep.tile([P, J * (N - NA)], BF16, name="ds_high", align_bytes=64)
+
+        def weave_high(engine_copy, s0, s1, pair):
+            weave_pair(engine_copy, ds_high[:, J * (s0 - NA) : J * (s1 - NA)], ds_rows[:, :, s0:s1], pair)
 
         def pool_copy(dst, src):
             nc.gpsimd.tensor_scalar(dst, src, 1.0, 0.0, ALU.mult, ALU.add)
@@ -179,18 +185,19 @@ def tile_attend_bwd_kernel(tc, doT, vT, p, delta, qm, offs, out):
 
         weigh(0, 0, N)
         weigh(1, 0, N)
-        weave_pair(nc.scalar.copy, ds_low[:], ds_rows[:, :, 0:NH], 0)
-        weave_pair(pool_copy, ds_high[:], ds_rows[:, :, NH:N], 0)
+        weave_pair(nc.scalar.copy, ds_low[:], ds_rows[:, :, 0:NA], 0)
+        weave_high(nc.scalar.copy, NA, NW, 0)
+        weave_high(pool_copy, NW, N, 0)
         weigh(2, 0, N)
         weigh(3, 0, NA)
         weigh(3, NA, N)
-        weave_pair(nc.scalar.copy, ds_high[:], ds_rows[:, :, NH:N], 1)
-        weave_pair(nc.vector.tensor_copy, ds_low[:, 0 : J * NA], ds_rows[:, :, 0:NA], 1)
-        weave_pair(nc.vector.tensor_copy, ds_low[:, J * NA : J * NH], ds_rows[:, :, NA:NH], 1)
-        quantise_ds(0, NA, ds_low[:, 0 : J * NA])
+        weave_high(nc.scalar.copy, NW, N, 1)
+        weave_pair(nc.vector.tensor_copy, ds_low[:], ds_rows[:, :, 0:NA], 1)
+        weave_high(nc.vector.tensor_copy, NA, NW, 1)
+        quantise_ds(0, NA, ds_low[:])
         keys_gradient(0, 0, 0, NA)
-        quantise_ds(NA, NH, ds_low[:, J * NA : J * NH])
-        quantise_ds(NH, N, ds_high[:])
+        quantise_ds(NA, NH, ds_high[:, 0 : J * (NH - NA)])
+        quantise_ds(NH, N, ds_high[:, J * (NH - NA) : J * (N - NA)])
         keys_gradient(1, FILL, NA, N)
         for c0, c1, d in dk_cols:
             nc.vector.tensor_copy(window[:].indirect(offsets[:, c0 // 16 : c1 // 16]), d[:])

@@ -22,7 +22,6 @@ N = 512
 T = 1024
 D = 128
 NA = 128
-NV = 384
 QH = Q // 2
 WEAVE_OUT = "p (c i j) -> p c j i"
 WEAVE_IN = "p j (c i) -> p c j i"
@@ -53,6 +52,9 @@ def tile_attend_bwd_kernel(tc, doT, vT, p, delta, qm, offs, out):
         qm_raw = keep.tile([P, J, D], F32, name="qm_raw")
         nc.sync.dma_start(out=qm_raw[:], in_=qm[0].rearrange("(p j) d -> p j d", j=J))
 
+        delta_col = keep.tile([P, J], F32, name="delta_col")
+        nc.sync.dma_start(out=delta_col[:], in_=delta[0].rearrange("(p j) o -> p (j o)", j=J))
+
         p_rows = p[0].rearrange("(p j) s -> p j s", j=J)
         p_raw = []
         for h in range(2):
@@ -60,8 +62,6 @@ def tile_attend_bwd_kernel(tc, doT, vT, p, delta, qm, offs, out):
             nc.sync.dma_start(out=t[:], in_=p_rows[:, 2 * h : 2 * h + 2, :])
             p_raw.append(t)
 
-        delta_col = keep.tile([P, J], F32, name="delta_col")
-        nc.scalar.dma_start(out=delta_col[:], in_=delta[0].rearrange("(p j) o -> p (j o)", j=J))
 
         window = keep.tile([P, T], F32, name="window")
         nc.gpsimd.memset(window[:], 0.0)
@@ -91,7 +91,7 @@ def tile_attend_bwd_kernel(tc, doT, vT, p, delta, qm, offs, out):
         do_cols = [keep.tile([P, 2 * J * P], BF16, name=f"do_cols{pair}", align_bytes=64) for pair in range(2)]
 
         MH = QH // J
-        MV = 16
+        MV = 40
 
         def weave_do(engine_copy, hs, ms, pair):
             engine_copy(
@@ -100,14 +100,20 @@ def tile_attend_bwd_kernel(tc, doT, vT, p, delta, qm, offs, out):
             )
 
         weave_do(nc.scalar.copy, slice(0, 1), slice(0, MH), 0)
-        weave_pair(nc.vector.tensor_copy, v_cols[:, 0 : J * NV], v_got[:, :, 0:NV], 1)
-        weave_pair(nc.scalar.copy, v_cols[:, J * NV : J * N], v_got[:, :, NV:N], 1)
-        weave_do(nc.vector.tensor_copy, slice(0, 2), slice(MH - MV, MH), 1)
+        weave_do(nc.scalar.copy, slice(0, 1), slice(0, MV), 1)
         v_codes = keep.tile([P, N], U32, name="v_codes", align_bytes=64)
         v_scales = keep.tile([P, N], U8, name="v_scales", align_bytes=64)
-        nc.vector.quantize_mx(out=v_codes[:].bitcast(E4M3X4), scales=v_scales[:], in_=v_cols[:])
+        for s0 in (0, N // 2):
+            weave_pair(nc.vector.tensor_copy, v_cols[:, J * s0 : J * (s0 + N // 2)], v_got[:, :, s0 : s0 + N // 2], 1)
+        for s0 in (0, N // 2):
+            nc.vector.quantize_mx(
+                out=v_codes[:, s0 : s0 + N // 2].bitcast(E4M3X4),
+                scales=v_scales[:, s0 : s0 + N // 2],
+                in_=v_cols[:, J * s0 : J * (s0 + N // 2)],
+            )
         weave_do(nc.scalar.copy, slice(1, 2), slice(0, MH), 0)
-        weave_do(nc.scalar.copy, slice(0, 2), slice(0, MH - MV), 1)
+        weave_do(nc.scalar.copy, slice(1, 2), slice(0, MV), 1)
+        weave_do(nc.scalar.copy, slice(0, 2), slice(MV, MH), 1)
 
         do_codes = keep.tile([P, Q], U32, name="do_codes", align_bytes=64)
         do_scales = keep.tile([P, Q], U8, name="do_scales", align_bytes=64)
@@ -117,6 +123,7 @@ def tile_attend_bwd_kernel(tc, doT, vT, p, delta, qm, offs, out):
         for t0, t1 in ((0, 1), (1, 2), (2, 4)):
             if t0 == 2:
                 nc.vector.tensor_copy(qm_cols.rearrange(WEAVE_OUT, i=4, j=J), qm_raw[:].rearrange(WEAVE_IN, i=4))
+                nc.vector.quantize_mx(out=qm_codes[:].bitcast(E4M3X4), scales=qm_scales[:], in_=qm_cols)
             nc.vector.quantize_mx(
                 out=do_codes[:, t0 * P : t1 * P].bitcast(E5M2X4),
                 scales=do_scales[:, t0 * P : t1 * P],
@@ -137,7 +144,6 @@ def tile_attend_bwd_kernel(tc, doT, vT, p, delta, qm, offs, out):
             )
             dp.append(bank)
 
-        nc.vector.quantize_mx(out=qm_codes[:].bitcast(E4M3X4), scales=qm_scales[:], in_=qm_cols)
 
         ds_rows = keep.tile([P, J, N], BF16, name="ds_rows")
 
@@ -190,12 +196,14 @@ def tile_attend_bwd_kernel(tc, doT, vT, p, delta, qm, offs, out):
         weave_high(pool_copy, NW, N, 0)
         weigh(2, 0, N)
         weigh(3, 0, NA)
-        weigh(3, NA, N)
+        weigh(3, NW, N)
         weave_high(nc.scalar.copy, NW, N, 1)
         weave_pair(nc.vector.tensor_copy, ds_low[:], ds_rows[:, :, 0:NA], 1)
-        weave_high(nc.vector.tensor_copy, NA, NW, 1)
+        weigh(3, NA, NW)
         quantise_ds(0, NA, ds_low[:])
         keys_gradient(0, 0, 0, NA)
+        weave_high(nc.vector.tensor_copy, NA, NH, 1)
+        weave_high(nc.vector.tensor_copy, NH, NW, 1)
         quantise_ds(NA, NH, ds_high[:, 0 : J * (NH - NA)])
         quantise_ds(NH, N, ds_high[:, J * (NH - NA) : J * (N - NA)])
         keys_gradient(1, FILL, NA, N)

@@ -22,6 +22,7 @@ N = 512
 T = 1024
 D = 128
 NA = 128
+VG = 128
 QH = Q // 2
 WEAVE_OUT = "p (c i j) -> p c j i"
 WEAVE_IN = "p j (c i) -> p c j i"
@@ -36,11 +37,11 @@ def tile_attend_bwd_kernel(tc, doT, vT, p, delta, qm, offs, out):
         offsets = keep.tile([P, N // 16], U16, name="offsets")
 
         v_rows = vT.rearrange("(p j) t -> p j t", j=J)
-        v_raw = []
-        for j in range(J):
+        v_raw = {}
+        for j in (0, 2, 1, 3):
             t = keep.tile([P, T], F32, name=f"v_raw{j}")
             nc.sync.dma_start(out=t[:], in_=v_rows[:, j, :])
-            v_raw.append(t)
+            v_raw[j] = t
             if j == 0:
                 nc.sync.dma_start(offsets[:], offs)
 
@@ -80,18 +81,18 @@ def tile_attend_bwd_kernel(tc, doT, vT, p, delta, qm, offs, out):
 
         v_cols = keep.tile([P, J * N], BF16, name="v_cols", align_bytes=64)
         v_lanes = v_cols[:].rearrange("p (s j) -> p s j", j=J)
-        v_cast = keep.tile([P, T], BF16, name="v_cast")
-        v_got = keep.tile([P, J, N], F32, name="v_got")
-        nc.vector.tensor_copy(v_lanes[:, :, 0], v_raw[0][:].indirect(offsets[:]))
-        nc.vector.tensor_copy(v_cast[:], v_raw[1][:])
-        nc.scalar.activation(v_lanes[:, :, 1], v_cast[:].indirect(offsets[:]), ACT.Copy)
-        for j in (2, 3):
-            nc.vector.tensor_copy(v_got[:, j, :], v_raw[j][:].indirect(offsets[:]))
+        for j, share in ((0, 320), (1, 640)):
+            v_cast = keep.tile([P, T], BF16, name=f"v_cast{j}")
+            nc.scalar.activation(v_cast[:, 0:share], v_raw[j][:, 0:share], ACT.Copy)
+            nc.vector.tensor_copy(v_cast[:, share:T], v_raw[j][:, share:T])
+            nc.scalar.activation(v_lanes[:, VG:N, j], v_cast[:].indirect(offsets[:, VG // 16 : N // 16]), ACT.Copy)
+            nc.vector.tensor_copy(v_lanes[:, 0:VG, j], v_raw[j][:].indirect(offsets[:, 0 : VG // 16]))
+            nc.vector.tensor_copy(v_lanes[:, :, j + 2], v_raw[j + 2][:].indirect(offsets[:]))
 
         do_cols = [keep.tile([P, 2 * J * P], BF16, name=f"do_cols{pair}", align_bytes=64) for pair in range(2)]
 
         MH = QH // J
-        MV = 40
+        MS = (40, 48)
 
         def weave_do(engine_copy, hs, ms, pair):
             engine_copy(
@@ -100,35 +101,33 @@ def tile_attend_bwd_kernel(tc, doT, vT, p, delta, qm, offs, out):
             )
 
         weave_do(nc.scalar.copy, slice(0, 1), slice(0, MH), 0)
-        weave_do(nc.scalar.copy, slice(0, 1), slice(0, MV), 1)
         v_codes = keep.tile([P, N], U32, name="v_codes", align_bytes=64)
         v_scales = keep.tile([P, N], U8, name="v_scales", align_bytes=64)
-        for s0 in (0, N // 2):
-            weave_pair(nc.vector.tensor_copy, v_cols[:, J * s0 : J * (s0 + N // 2)], v_got[:, :, s0 : s0 + N // 2], 1)
         for s0 in (0, N // 2):
             nc.vector.quantize_mx(
                 out=v_codes[:, s0 : s0 + N // 2].bitcast(E4M3X4),
                 scales=v_scales[:, s0 : s0 + N // 2],
                 in_=v_cols[:, J * s0 : J * (s0 + N // 2)],
             )
-        weave_do(nc.scalar.copy, slice(1, 2), slice(0, MH), 0)
-        weave_do(nc.scalar.copy, slice(1, 2), slice(0, MV), 1)
-        weave_do(nc.scalar.copy, slice(0, 2), slice(MV, MH), 1)
+        weave_do(nc.vector.tensor_copy, slice(0, 1), slice(0, MH), 1)
+        for pair in range(2):
+            weave_do(nc.scalar.copy, slice(1, 2), slice(0, MS[pair]), pair)
+            weave_do(nc.vector.tensor_copy, slice(1, 2), slice(MS[pair], MH), pair)
 
         do_codes = keep.tile([P, Q], U32, name="do_codes", align_bytes=64)
         do_scales = keep.tile([P, Q], U8, name="do_scales", align_bytes=64)
         qm_cols = do_cols[0][:, 0 : J * D]
-        qm_codes = keep.tile([P, D], U32, name="qm_codes", align_bytes=64)
         qm_scales = keep.tile([P, D], U8, name="qm_scales", align_bytes=64)
+        qm_codes = keep.tile([P, D], U32, name="qm_codes", align_bytes=64)
         for t0, t1 in ((0, 1), (1, 2), (2, 4)):
             if t0 == 2:
                 nc.vector.tensor_copy(qm_cols.rearrange(WEAVE_OUT, i=4, j=J), qm_raw[:].rearrange(WEAVE_IN, i=4))
-                nc.vector.quantize_mx(out=qm_codes[:].bitcast(E4M3X4), scales=qm_scales[:], in_=qm_cols)
             nc.vector.quantize_mx(
                 out=do_codes[:, t0 * P : t1 * P].bitcast(E5M2X4),
                 scales=do_scales[:, t0 * P : t1 * P],
                 in_=do_cols[t0 // 2][:, t0 % 2 * P * J : (t0 % 2 + t1 - t0) * P * J],
             )
+        nc.vector.quantize_mx(out=qm_codes[:].bitcast(E4M3X4), scales=qm_scales[:], in_=qm_cols)
         dp = []
         for t in range(J):
             cols = slice(t * P, (t + 1) * P)

@@ -58,9 +58,9 @@ def tile_attend_bwd_kernel(tc, doT, vT, p, delta, qm, offs, out):
 
         p_rows = p[0].rearrange("(p j) s -> p j s", j=J)
         p_raw = []
-        for h in range(2):
-            t = keep.tile([P, 2, N], F32, name=f"p_raw{h}")
-            nc.sync.dma_start(out=t[:], in_=p_rows[:, 2 * h : 2 * h + 2, :])
+        for j in range(J):
+            t = keep.tile([P, N], F32, name=f"p_raw{j}")
+            nc.sync.dma_start(out=t[:], in_=p_rows[:, j, :])
             p_raw.append(t)
 
 
@@ -87,20 +87,30 @@ def tile_attend_bwd_kernel(tc, doT, vT, p, delta, qm, offs, out):
             nc.vector.tensor_copy(v_cast[:, share:T], v_raw[j][:, share:T])
             nc.scalar.activation(v_lanes[:, VG:N, j], v_cast[:].indirect(offsets[:, VG // 16 : N // 16]), ACT.Copy)
             nc.vector.tensor_copy(v_lanes[:, 0:VG, j], v_raw[j][:].indirect(offsets[:, 0 : VG // 16]))
-            nc.vector.tensor_copy(v_lanes[:, :, j + 2], v_raw[j + 2][:].indirect(offsets[:]))
+            for s0, s1 in ((0, N),) if j == 0 else ((0, N // 2), (N // 2, N)):
+                nc.vector.tensor_copy(v_lanes[:, s0:s1, j + 2], v_raw[j + 2][:].indirect(offsets[:, s0 // 16 : s1 // 16]))
 
-        do_cols = [keep.tile([P, 2 * J * P], BF16, name=f"do_cols{pair}", align_bytes=64) for pair in range(2)]
-
+        do_cols = keep.tile([P, J * J * P], BF16, name="do_cols", align_bytes=64)
         MH = QH // J
-        MS = (40, 48)
+        MV = 44
 
-        def weave_do(engine_copy, hs, ms, pair):
+        def weave_do(engine_copy, h, ms, ts):
             engine_copy(
-                do_cols[pair][:].rearrange("p (t h m j) -> p h m j t", t=2, h=2, j=J)[:, hs, ms, :, :],
-                do_raw[:].rearrange("p h j (m t) -> p h m j t", t=J)[:, hs, ms, :, 2 * pair : 2 * pair + 2],
+                do_cols[:].rearrange("p (t h m j) -> p h m j t", t=J, h=2, j=J)[:, h, ms, :, ts],
+                do_raw[:].rearrange("p h j (m t) -> p h m j t", t=J)[:, h, ms, :, ts],
             )
 
-        weave_do(nc.scalar.copy, slice(0, 1), slice(0, MH), 0)
+        do_codes = keep.tile([P, Q], U32, name="do_codes", align_bytes=64)
+        do_scales = keep.tile([P, Q], U8, name="do_scales", align_bytes=64)
+
+        def quantise_do(c0, c1):
+            nc.vector.quantize_mx(
+                out=do_codes[:, c0:c1].bitcast(E5M2X4),
+                scales=do_scales[:, c0:c1],
+                in_=do_cols[:, J * c0 : J * c1],
+            )
+
+        weave_do(nc.scalar.copy, 0, slice(0, MH), slice(0, J))
         v_codes = keep.tile([P, N], U32, name="v_codes", align_bytes=64)
         v_scales = keep.tile([P, N], U8, name="v_scales", align_bytes=64)
         for s0 in (0, N // 2):
@@ -109,24 +119,19 @@ def tile_attend_bwd_kernel(tc, doT, vT, p, delta, qm, offs, out):
                 scales=v_scales[:, s0 : s0 + N // 2],
                 in_=v_cols[:, J * s0 : J * (s0 + N // 2)],
             )
-        weave_do(nc.vector.tensor_copy, slice(0, 1), slice(0, MH), 1)
-        for pair in range(2):
-            weave_do(nc.scalar.copy, slice(1, 2), slice(0, MS[pair]), pair)
-            weave_do(nc.vector.tensor_copy, slice(1, 2), slice(MS[pair], MH), pair)
+        weave_do(nc.scalar.copy, 1, slice(MV, MH), slice(0, 2))
+        weave_do(nc.vector.tensor_copy, 1, slice(0, MV), slice(0, 2))
+        weave_do(nc.scalar.copy, 1, slice(0, MH), slice(2, J))
 
-        do_codes = keep.tile([P, Q], U32, name="do_codes", align_bytes=64)
-        do_scales = keep.tile([P, Q], U8, name="do_scales", align_bytes=64)
-        qm_cols = do_cols[0][:, 0 : J * D]
+        qm_cols = do_cols[:, 0 : J * D]
         qm_scales = keep.tile([P, D], U8, name="qm_scales", align_bytes=64)
         qm_codes = keep.tile([P, D], U32, name="qm_codes", align_bytes=64)
-        for t0, t1 in ((0, 1), (1, 2), (2, 4)):
-            if t0 == 2:
-                nc.vector.tensor_copy(qm_cols.rearrange(WEAVE_OUT, i=4, j=J), qm_raw[:].rearrange(WEAVE_IN, i=4))
-            nc.vector.quantize_mx(
-                out=do_codes[:, t0 * P : t1 * P].bitcast(E5M2X4),
-                scales=do_scales[:, t0 * P : t1 * P],
-                in_=do_cols[t0 // 2][:, t0 % 2 * P * J : (t0 % 2 + t1 - t0) * P * J],
-            )
+        quantise_do(0, MH)
+        quantise_do(P, P + MH)
+        quantise_do(MH, P)
+        quantise_do(P + MH, 2 * P)
+        nc.vector.tensor_copy(qm_cols.rearrange(WEAVE_OUT, i=4, j=J), qm_raw[:].rearrange(WEAVE_IN, i=4))
+        quantise_do(2 * P, 4 * P)
         nc.vector.quantize_mx(out=qm_codes[:].bitcast(E4M3X4), scales=qm_scales[:], in_=qm_cols)
         dp = []
         for t in range(J):
@@ -151,7 +156,7 @@ def tile_attend_bwd_kernel(tc, doT, vT, p, delta, qm, offs, out):
                 ds_rows[:, t, s0:s1],
                 dp[t][:, s0:s1],
                 delta_col[:, t : t + 1],
-                p_raw[t // 2][:, t % 2, s0:s1],
+                p_raw[t][:, s0:s1],
                 ALU.subtract,
                 ALU.mult,
             )

@@ -81,10 +81,11 @@ def tile_attend_bwd_kernel(tc, doT, vT, p, delta, qm, offs, out):
 
         v_cols = keep.tile([P, J * N], BF16, name="v_cols", align_bytes=64)
         v_lanes = v_cols[:].rearrange("p (s j) -> p s j", j=J)
-        for j, share in ((0, 320), (1, 640)):
+        for j, share in ((0, 320), (1, T)):
             v_cast = keep.tile([P, T], BF16, name=f"v_cast{j}")
             nc.scalar.activation(v_cast[:, 0:share], v_raw[j][:, 0:share], ACT.Copy)
-            nc.vector.tensor_copy(v_cast[:, share:T], v_raw[j][:, share:T])
+            if share < T:
+                nc.vector.tensor_copy(v_cast[:, share:T], v_raw[j][:, share:T])
             nc.scalar.activation(v_lanes[:, VG:N, j], v_cast[:].indirect(offsets[:, VG // 16 : N // 16]), ACT.Copy)
             nc.vector.tensor_copy(v_lanes[:, 0:VG, j], v_raw[j][:].indirect(offsets[:, 0 : VG // 16]))
             for s0, s1 in ((0, N),) if j == 0 else ((0, N // 2), (N // 2, N)):
@@ -92,7 +93,11 @@ def tile_attend_bwd_kernel(tc, doT, vT, p, delta, qm, offs, out):
 
         do_cols = keep.tile([P, J * J * P], BF16, name="do_cols", align_bytes=64)
         MH = QH // J
-        MV = 44
+        MV = 40
+        MG = 24
+
+        def pool_copy(dst, src):
+            nc.gpsimd.tensor_scalar(dst, src, 1.0, 0.0, ALU.mult, ALU.add)
 
         def weave_do(engine_copy, h, ms, ts):
             engine_copy(
@@ -110,7 +115,11 @@ def tile_attend_bwd_kernel(tc, doT, vT, p, delta, qm, offs, out):
                 in_=do_cols[:, J * c0 : J * c1],
             )
 
-        weave_do(nc.scalar.copy, 0, slice(0, MH), slice(0, J))
+        pool_copy(
+            do_cols[:].rearrange("p (t h m j) -> p h m t j", t=J, h=2, j=J)[:, 0, 0:MG, :, :],
+            do_raw[:].rearrange("p h j (m t) -> p h m t j", t=J)[:, 0, 0:MG, :, :],
+        )
+        weave_do(nc.scalar.copy, 0, slice(MG, MH), slice(0, J))
         v_codes = keep.tile([P, N], U32, name="v_codes", align_bytes=64)
         v_scales = keep.tile([P, N], U8, name="v_scales", align_bytes=64)
         for s0 in (0, N // 2):
@@ -168,9 +177,6 @@ def tile_attend_bwd_kernel(tc, doT, vT, p, delta, qm, offs, out):
 
         def weave_high(engine_copy, s0, s1, pair):
             weave_pair(engine_copy, ds_high[:, J * (s0 - NA) : J * (s1 - NA)], ds_rows[:, :, s0:s1], pair)
-
-        def pool_copy(dst, src):
-            nc.gpsimd.tensor_scalar(dst, src, 1.0, 0.0, ALU.mult, ALU.add)
 
         def quantise_ds(s0, s1, src):
             cols = slice(FILL + s0, FILL + s1)

@@ -16,207 +16,199 @@ ACT = mybir.ActivationFunctionType
 
 P = 128
 J = 4
-E = 512
 Q = 512
 N = 512
 T = 1024
 D = 128
-NA = 128
-VG = 128
+C = 128
 QH = Q // 2
 WEAVE_OUT = "p (c i j) -> p c j i"
 WEAVE_IN = "p j (c i) -> p c j i"
+NV = 256
+TAGS = ("ds_a", "ds_b", "ds_c", "ds_d")
 
 
 def tile_attend_bwd_kernel(tc, doT, vT, p, delta, qm, offs, out):
     nc = tc.nc
     with ExitStack() as ctx:
         keep = ctx.enter_context(tc.tile_pool(name="keep", bufs=1))
+        reused = ctx.enter_context(tc.tile_pool(name="reused", bufs=1))
         psum = ctx.enter_context(tc.psum_pool(name="psum", bufs=1))
 
-        offsets = keep.tile([P, N // 16], U16, name="offsets")
+        def listed(s0, s1):
+            return offsets[:, s0 // 16 : s1 // 16]
 
+        def weave(engine_copy, dst, src, j0, j1):
+            engine_copy(
+                dst.rearrange(WEAVE_OUT, i=4, j=J)[:, :, j0:j1, :],
+                src[:, j0:j1, :].rearrange(WEAVE_IN, i=4),
+            )
+
+        def scalar_cast(dst, src):
+            nc.scalar.activation(dst, src, ACT.Copy)
+
+        offsets = keep.tile([P, N // 16], U16, name="offsets")
+        do_rows = doT[0].rearrange("(p j) q -> p j q", j=J)
+        do_raw = []
+        for h in range(2):
+            t = keep.tile([P, J, QH], F32, name=f"do_raw{h}")
+            nc.sync.dma_start(out=t[:], in_=do_rows[:, :, h * QH : (h + 1) * QH])
+            do_raw.append(t)
+        nc.sync.dma_start(offsets[:], offs)
         v_rows = vT.rearrange("(p j) t -> p j t", j=J)
-        v_raw = {}
-        for j in (0, 2, 1, 3):
+        v_raw = []
+        for j in range(J):
             t = keep.tile([P, T], F32, name=f"v_raw{j}")
             nc.sync.dma_start(out=t[:], in_=v_rows[:, j, :])
-            v_raw[j] = t
-            if j == 0:
-                nc.sync.dma_start(offsets[:], offs)
-
-        do_rows = doT[0].rearrange("(p j) q -> p j q", j=J)
-        do_raw = keep.tile([P, 2, J, QH], F32, name="do_raw")
-        for h in range(2):
-            nc.sync.dma_start(out=do_raw[:, h, :, :], in_=do_rows[:, :, h * QH : (h + 1) * QH])
-
+            v_raw.append(t)
         qm_raw = keep.tile([P, J, D], F32, name="qm_raw")
         nc.sync.dma_start(out=qm_raw[:], in_=qm[0].rearrange("(p j) d -> p j d", j=J))
-
         delta_col = keep.tile([P, J], F32, name="delta_col")
         nc.sync.dma_start(out=delta_col[:], in_=delta[0].rearrange("(p j) o -> p (j o)", j=J))
-
         p_rows = p[0].rearrange("(p j) s -> p j s", j=J)
         p_raw = []
-        for j in range(J):
-            t = keep.tile([P, N], F32, name=f"p_raw{j}")
-            nc.sync.dma_start(out=t[:], in_=p_rows[:, j, :])
-            p_raw.append(t)
-
+        for s0, s1 in ((0, C), (C, 2 * C), (2 * C, N)):
+            if s0 == 0:
+                t = reused.tile([P, J, C], F32, name="p_first", align_bytes=64, offset=0)
+            else:
+                t = keep.tile([P, J, s1 - s0], F32, name=f"p_raw{s0}")
+            nc.sync.dma_start(out=t[:], in_=p_rows[:, :, s0:s1])
+            for c0 in range(0, s1 - s0, C):
+                p_raw.append(t[:, :, c0 : c0 + C])
 
         window = keep.tile([P, T], F32, name="window")
         nc.gpsimd.memset(window[:], 0.0)
-        FILL = N - NA
-        ds_codes = keep.tile([P, FILL + N], U32, name="ds_codes", align_bytes=64)
-        ds_scales = keep.tile([P, FILL + N], U8, name="ds_scales", align_bytes=64)
-        nc.gpsimd.memset(ds_codes[:, 0:FILL], 0)
-        nc.gpsimd.memset(ds_scales[:, 0:FILL].bitcast(U32), 0)
 
-        def weave_pair(engine_copy, dst, src, pair):
-            js = slice(2 * pair, 2 * pair + 2)
-            engine_copy(
-                dst.rearrange(WEAVE_OUT, i=4, j=J)[:, :, js, :],
-                src[:, js, :].rearrange(WEAVE_IN, i=4),
-            )
-
-        v_cols = keep.tile([P, J * N], BF16, name="v_cols", align_bytes=64)
-        v_lanes = v_cols[:].rearrange("p (s j) -> p s j", j=J)
-        for j, share in ((0, 320), (1, T)):
-            v_cast = keep.tile([P, T], BF16, name=f"v_cast{j}")
-            nc.scalar.activation(v_cast[:, 0:share], v_raw[j][:, 0:share], ACT.Copy)
-            if share < T:
-                nc.vector.tensor_copy(v_cast[:, share:T], v_raw[j][:, share:T])
-            nc.scalar.activation(v_lanes[:, VG:N, j], v_cast[:].indirect(offsets[:, VG // 16 : N // 16]), ACT.Copy)
-            nc.vector.tensor_copy(v_lanes[:, 0:VG, j], v_raw[j][:].indirect(offsets[:, 0 : VG // 16]))
-            for s0, s1 in ((0, N),) if j == 0 else ((0, N // 2), (N // 2, N)):
-                nc.vector.tensor_copy(v_lanes[:, s0:s1, j + 2], v_raw[j + 2][:].indirect(offsets[:, s0 // 16 : s1 // 16]))
-
-        do_cols = keep.tile([P, J * J * P], BF16, name="do_cols", align_bytes=64)
-        MH = QH // J
-        MV = 40
-        MG = 24
-
-        def pool_copy(dst, src):
-            nc.gpsimd.tensor_scalar(dst, src, 1.0, 0.0, ALU.mult, ALU.add)
-
-        def weave_do(engine_copy, h, ms, ts):
-            engine_copy(
-                do_cols[:].rearrange("p (t h m j) -> p h m j t", t=J, h=2, j=J)[:, h, ms, :, ts],
-                do_raw[:].rearrange("p h j (m t) -> p h m j t", t=J)[:, h, ms, :, ts],
-            )
-
+        do_cols = keep.tile([P, J * Q], BF16, name="do_cols", align_bytes=64)
         do_codes = keep.tile([P, Q], U32, name="do_codes", align_bytes=64)
         do_scales = keep.tile([P, Q], U8, name="do_scales", align_bytes=64)
-
-        def quantise_do(c0, c1):
-            nc.vector.quantize_mx(
-                out=do_codes[:, c0:c1].bitcast(E5M2X4),
-                scales=do_scales[:, c0:c1],
-                in_=do_cols[:, J * c0 : J * c1],
+        for h, engine_copy in enumerate((scalar_cast, nc.vector.tensor_copy)):
+            engine_copy(
+                do_cols[:].rearrange("p (t h m j) -> p h m j t", t=J, h=2, j=J)[:, h, :, :, :],
+                do_raw[h][:].rearrange("p j (m t) -> p m j t", t=J),
             )
+        nc.vector.quantize_mx(out=do_codes[:].bitcast(E5M2X4), scales=do_scales[:], in_=do_cols[:])
 
-        pool_copy(
-            do_cols[:].rearrange("p (t h m j) -> p h m t j", t=J, h=2, j=J)[:, 0, 0:MG, :, :],
-            do_raw[:].rearrange("p h j (m t) -> p h m t j", t=J)[:, 0, 0:MG, :, :],
-        )
-        weave_do(nc.scalar.copy, 0, slice(MG, MH), slice(0, J))
-        v_codes = keep.tile([P, N], U32, name="v_codes", align_bytes=64)
+        v_low = keep.tile([P, J * NV], BF16, name="v_low", align_bytes=64)
+        v_lanes = v_low[:].rearrange("p (s j) -> p s j", j=J)
+        v_high = keep.tile([P, J * (N - NV)], BF16, name="v_high", align_bytes=64)
+        v_picked = keep.tile([P, J, N - NV], BF16, name="v_picked")
+        v_codes = {}
         v_scales = keep.tile([P, N], U8, name="v_scales", align_bytes=64)
-        for s0 in (0, N // 2):
-            nc.vector.quantize_mx(
-                out=v_codes[:, s0 : s0 + N // 2].bitcast(E4M3X4),
-                scales=v_scales[:, s0 : s0 + N // 2],
-                in_=v_cols[:, J * s0 : J * (s0 + N // 2)],
-            )
-        weave_do(nc.scalar.copy, 1, slice(MV, MH), slice(0, 2))
-        weave_do(nc.vector.tensor_copy, 1, slice(0, MV), slice(0, 2))
-        weave_do(nc.scalar.copy, 1, slice(0, MH), slice(2, J))
 
-        qm_cols = do_cols[:, 0 : J * D]
+        def quantise_v(s0, s1, src):
+            if s1 == N:
+                codes = reused.tile([P, C], U32, name="v_codes_last", align_bytes=64, offset=0)
+            else:
+                codes = keep.tile([P, C], U32, name=f"v_codes{s0}", align_bytes=64)
+            v_codes[s0 // C] = codes
+            nc.vector.quantize_mx(out=codes[:].bitcast(E4M3X4), scales=v_scales[:, s0:s1], in_=src)
+
+        for j in range(J - 1):
+            nc.scalar.activation(v_picked[:, j, :], v_raw[j][:].indirect(listed(NV, N)), ACT.Copy)
+            nc.vector.tensor_copy(v_lanes[:, :, j], v_raw[j][:].indirect(listed(0, NV)))
+            if j == 1:
+                weave(nc.vector.tensor_copy, v_high[:, 0 : J * C], v_picked[:, :, 0:C], 0, 2)
+                weave(nc.scalar.copy, v_high[:, J * C : 2 * J * C], v_picked[:, :, C : 2 * C], 0, 2)
+        for s0 in range(0, N - NV, C):
+            nc.scalar.activation(
+                v_picked[:, J - 1, s0 : s0 + C], v_raw[J - 1][:].indirect(listed(NV + s0, NV + s0 + C)), ACT.Copy
+            )
+            weave(nc.scalar.copy, v_high[:, J * s0 : J * (s0 + C)], v_picked[:, :, s0 : s0 + C], 2, J)
+        for s0 in range(0, NV, C):
+            nc.vector.tensor_copy(v_lanes[:, s0 : s0 + C, J - 1], v_raw[J - 1][:].indirect(listed(s0, s0 + C)))
+            quantise_v(s0, s0 + C, v_low[:, J * s0 : J * (s0 + C)])
+
+        quantise_v(2 * C, 3 * C, v_high[:, 0 : J * C])
+        qm_cols = keep.tile([P, J * D], BF16, name="qm_cols", align_bytes=64)
+        qm_codes = reused.tile([P, D], U32, name="qm_codes", align_bytes=64, offset=4 * C)
         qm_scales = keep.tile([P, D], U8, name="qm_scales", align_bytes=64)
-        qm_codes = keep.tile([P, D], U32, name="qm_codes", align_bytes=64)
-        quantise_do(0, MH)
-        quantise_do(P, P + MH)
-        quantise_do(MH, P)
-        quantise_do(P + MH, 2 * P)
-        nc.vector.tensor_copy(qm_cols.rearrange(WEAVE_OUT, i=4, j=J), qm_raw[:].rearrange(WEAVE_IN, i=4))
-        quantise_do(2 * P, 4 * P)
-        nc.vector.quantize_mx(out=qm_codes[:].bitcast(E4M3X4), scales=qm_scales[:], in_=qm_cols)
-        dp = []
-        for t in range(J):
+        weave(nc.vector.tensor_copy, qm_cols[:], qm_raw, 0, J)
+
+        def dp_pass(dst, c, t):
             cols = slice(t * P, (t + 1) * P)
-            bank = psum.tile([P, N], F32, name=f"dp{t}")
+            slots = slice(c * C, (c + 1) * C)
             nc.tensor.matmul_mx(
-                out=bank[:],
+                out=dst,
                 lhsT=do_codes[:, cols].bitcast(E5M2X4),
                 lhsT_scale=do_scales[:, cols],
-                rhs=v_codes[:].bitcast(E4M3X4),
-                rhs_scale=v_scales[:],
+                rhs=v_codes[c][:].bitcast(E4M3X4),
+                rhs_scale=v_scales[:, slots],
                 start=True,
                 stop=True,
             )
-            dp.append(bank)
 
+        dp = {}
 
-        ds_rows = keep.tile([P, J, N], BF16, name="ds_rows")
+        def scores_gradient(c):
+            if c == 0:
+                for t in range(J):
+                    bank = psum.tile([P, C], F32, name=f"first{t}", tag=f"bank{t}")
+                    dp[c, t] = bank[:]
+            else:
+                bank = psum.tile([P, J, C], F32, name=f"dp{c}", tag=f"bank{J - 1 + c}")
+                for t in range(J):
+                    dp[c, t] = bank[:, t, :]
+            for t in range(J):
+                dp_pass(dp[c, t], c, t)
 
-        def weigh(t, s0, s1):
-            nc.vector.scalar_tensor_tensor(
-                ds_rows[:, t, s0:s1],
-                dp[t][:, s0:s1],
-                delta_col[:, t : t + 1],
-                p_raw[t][:, s0:s1],
-                ALU.subtract,
-                ALU.mult,
-            )
+        ds_rows = [keep.tile([P, J, C], BF16, name=f"ds_rows{c}") for c in range(J)]
+        ds_cols = {}
+        dk_cols = [keep.tile([P, C], F32, name=f"dk_cols{c}") for c in range(J)]
+        dk = {}
 
-        NH = N // 2
-        NW = 320
-        ds_low = keep.tile([P, J * NA], BF16, name="ds_low", align_bytes=64)
-        ds_high = keep.tile([P, J * (N - NA)], BF16, name="ds_high", align_bytes=64)
+        def weigh(c, t0, t1):
+            for t in range(t0, t1):
+                nc.vector.scalar_tensor_tensor(
+                    ds_rows[c][:, t, :], dp[c, t], delta_col[:, t : t + 1], p_raw[c][:, t, :], ALU.subtract, ALU.mult
+                )
 
-        def weave_high(engine_copy, s0, s1, pair):
-            weave_pair(engine_copy, ds_high[:, J * (s0 - NA) : J * (s1 - NA)], ds_rows[:, :, s0:s1], pair)
+        def weave_ds(engine_copy, c, j0, j1):
+            if j0 == 0:
+                ds_cols[c] = keep.tile([P, J * C], BF16, name=f"ds_cols{c}", tag=TAGS[c], align_bytes=64)
+            weave(engine_copy, ds_cols[c][:], ds_rows[c], j0, j1)
 
-        def quantise_ds(s0, s1, src):
-            cols = slice(FILL + s0, FILL + s1)
-            nc.vector.quantize_mx(out=ds_codes[:, cols].bitcast(E5M2X4), scales=ds_scales[:, cols], in_=src)
-
-        dk_cols = []
-
-        def keys_gradient(h, first, c0, c1):
-            dk = psum.tile([P, N], F32, name=f"dk{h}")
+        def keys_gradient(c):
+            codes = keep.tile([P, C], U32, name=f"ds_codes{c}", align_bytes=64)
+            scales = keep.tile([P, C], U8, name=f"ds_scales{c}", align_bytes=64)
+            nc.vector.quantize_mx(out=codes[:].bitcast(E5M2X4), scales=scales[:], in_=ds_cols[c][:])
+            bank = psum.tile([P, C], F32, name=f"dk{c}", tag=f"bank{(c + 7) % 8}")
             nc.tensor.matmul_mx(
-                out=dk[:],
+                out=bank[:],
                 lhsT=qm_codes[:].bitcast(E4M3X4),
                 lhsT_scale=qm_scales[:],
-                rhs=ds_codes[:, first : first + N].bitcast(E5M2X4),
-                rhs_scale=ds_scales[:, first : first + N],
+                rhs=codes[:].bitcast(E5M2X4),
+                rhs_scale=scales[:],
                 start=True,
                 stop=True,
             )
-            d = keep.tile([P, c1 - c0], F32, name=f"dk_cols{c0}")
-            nc.scalar.copy(d[:], dk[:, FILL - first + c0 : FILL - first + c1])
-            dk_cols.append((c0, c1, d))
+            dk[c] = bank
 
-        weigh(0, 0, N)
-        weigh(1, 0, N)
-        weave_pair(nc.scalar.copy, ds_low[:], ds_rows[:, :, 0:NA], 0)
-        weave_high(nc.scalar.copy, NA, NW, 0)
-        weave_high(pool_copy, NW, N, 0)
-        weigh(2, 0, N)
-        weigh(3, 0, NA)
-        weigh(3, NW, N)
-        weave_high(nc.scalar.copy, NW, N, 1)
-        weave_pair(nc.vector.tensor_copy, ds_low[:], ds_rows[:, :, 0:NA], 1)
-        weigh(3, NA, NW)
-        quantise_ds(0, NA, ds_low[:])
-        keys_gradient(0, 0, 0, NA)
-        weave_high(nc.vector.tensor_copy, NA, NH, 1)
-        weave_high(nc.vector.tensor_copy, NH, NW, 1)
-        quantise_ds(NA, NH, ds_high[:, 0 : J * (NH - NA)])
-        quantise_ds(NH, N, ds_high[:, J * (NH - NA) : J * (N - NA)])
-        keys_gradient(1, FILL, NA, N)
-        for c0, c1, d in dk_cols:
-            nc.vector.tensor_copy(window[:].indirect(offsets[:, c0 // 16 : c1 // 16]), d[:])
+        def place(engine_copy, c):
+            engine_copy(dk_cols[c][:], dk[c][:])
+            nc.scalar.activation(window[:].indirect(listed(c * C, (c + 1) * C)), dk_cols[c][:], ACT.Copy)
+
+        scores_gradient(0)
+        scores_gradient(1)
+        scores_gradient(2)
+        for c in range(2):
+            weigh(c, 0, 2)
+            weave_ds(nc.scalar.copy, c, 0, 2)
+            weigh(c, 2, J)
+            weave_ds(nc.scalar.copy, c, 2, J)
+        nc.vector.quantize_mx(out=qm_codes[:].bitcast(E4M3X4), scales=qm_scales[:], in_=qm_cols[:])
+        keys_gradient(0)
+        place(nc.scalar.copy, 0)
+        quantise_v(3 * C, N, v_high[:, J * C : 2 * J * C])
+        scores_gradient(3)
+        keys_gradient(1)
+        place(nc.vector.tensor_copy, 1)
+        weigh(2, 0, J)
+        weave_ds(nc.vector.tensor_copy, 2, 0, J)
+        keys_gradient(2)
+        place(nc.vector.tensor_copy, 2)
+        weigh(3, 0, J)
+        weave_ds(nc.vector.tensor_copy, 3, 0, J)
+        keys_gradient(3)
+        place(nc.vector.tensor_copy, 3)
         nc.sync.dma_start(out=out, in_=window[:])

@@ -82,12 +82,21 @@ def tile_attend_bwd_kernel(tc, doT, vT, p, delta, qm, offs, out):
         do_cols = keep.tile([P, J * Q], BF16, name="do_cols", align_bytes=64)
         do_codes = keep.tile([P, Q], U32, name="do_codes", align_bytes=64)
         do_scales = keep.tile([P, Q], U8, name="do_scales", align_bytes=64)
-        for h, engine_copy in enumerate((scalar_cast, nc.vector.tensor_copy)):
+
+        def weave_do(engine_copy, h, t0, t1):
             engine_copy(
-                do_cols[:].rearrange("p (t h m j) -> p h m j t", t=J, h=2, j=J)[:, h, :, :, :],
-                do_raw[h][:].rearrange("p j (m t) -> p m j t", t=J),
+                do_cols[:].rearrange("p (t h m j) -> p h m j t", t=J, h=2, j=J)[:, h, :, :, t0:t1],
+                do_raw[h][:].rearrange("p j (m t) -> p m j t", t=J)[:, :, :, t0:t1],
             )
-        nc.vector.quantize_mx(out=do_codes[:].bitcast(E5M2X4), scales=do_scales[:], in_=do_cols[:])
+
+        weave_do(scalar_cast, 0, 0, J)
+        weave_do(nc.vector.tensor_copy, 1, 0, 2)
+        weave_do(scalar_cast, 1, 2, J)
+        for c0 in (0, QH):
+            cols = slice(c0, c0 + QH)
+            nc.vector.quantize_mx(
+                out=do_codes[:, cols].bitcast(E5M2X4), scales=do_scales[:, cols], in_=do_cols[:, J * c0 : J * (c0 + QH)]
+            )
 
         v_low = keep.tile([P, J * NV], BF16, name="v_low", align_bytes=64)
         v_lanes = v_low[:].rearrange("p (s j) -> p s j", j=J)
@@ -108,8 +117,7 @@ def tile_attend_bwd_kernel(tc, doT, vT, p, delta, qm, offs, out):
             nc.scalar.activation(v_picked[:, j, :], v_raw[j][:].indirect(listed(NV, N)), ACT.Copy)
             nc.vector.tensor_copy(v_lanes[:, :, j], v_raw[j][:].indirect(listed(0, NV)))
             if j == 1:
-                weave(nc.vector.tensor_copy, v_high[:, 0 : J * C], v_picked[:, :, 0:C], 0, 2)
-                weave(nc.scalar.copy, v_high[:, J * C : 2 * J * C], v_picked[:, :, C : 2 * C], 0, 2)
+                weave(nc.scalar.copy, v_high[:], v_picked, 0, 2)
         for s0 in range(0, N - NV, C):
             nc.scalar.activation(
                 v_picked[:, J - 1, s0 : s0 + C], v_raw[J - 1][:].indirect(listed(NV + s0, NV + s0 + C)), ACT.Copy
@@ -202,13 +210,13 @@ def tile_attend_bwd_kernel(tc, doT, vT, p, delta, qm, offs, out):
         quantise_v(3 * C, N, v_high[:, J * C : 2 * J * C])
         scores_gradient(3)
         keys_gradient(1)
-        place(nc.vector.tensor_copy, 1)
+        place(nc.scalar.copy, 1)
         weigh(2, 0, J)
         weave_ds(nc.vector.tensor_copy, 2, 0, J)
         keys_gradient(2)
-        place(nc.vector.tensor_copy, 2)
         weigh(3, 0, J)
         weave_ds(nc.vector.tensor_copy, 3, 0, J)
+        place(nc.vector.tensor_copy, 2)
         keys_gradient(3)
         place(nc.vector.tensor_copy, 3)
         nc.sync.dma_start(out=out, in_=window[:])

@@ -25,7 +25,7 @@ QH = Q // 2
 WEAVE_OUT = "p (c i j) -> p c j i"
 WEAVE_IN = "p j (c i) -> p c j i"
 NV = 256
-TAGS = ("ds_a", "ds_b", "ds_c", "ds_d")
+TAGS = ("ds_a", "ds_b", "ds_b", "ds_d")
 
 
 def tile_attend_bwd_kernel(tc, doT, vT, p, delta, qm, offs, out):
@@ -171,6 +171,9 @@ def tile_attend_bwd_kernel(tc, doT, vT, p, delta, qm, offs, out):
                     ds_rows[c][:, t, :], dp[c, t], delta_col[:, t : t + 1], p_raw[c][:, t, :], ALU.subtract, ALU.mult
                 )
 
+        def pool_copy(dst, src):
+            nc.gpsimd.tensor_scalar(dst, src, 1.0, 0.0, ALU.mult, ALU.add)
+
         def weave_ds(engine_copy, c, j0, j1):
             if j0 == 0:
                 ds_cols[c] = keep.tile([P, J * C], BF16, name=f"ds_cols{c}", tag=TAGS[c], align_bytes=64)
@@ -209,14 +212,15 @@ def tile_attend_bwd_kernel(tc, doT, vT, p, delta, qm, offs, out):
         place(nc.scalar.copy, 0)
         quantise_v(3 * C, N, v_high[:, J * C : 2 * J * C])
         scores_gradient(3)
-        keys_gradient(1)
-        place(nc.scalar.copy, 1)
         weigh(2, 0, J)
-        weave_ds(nc.vector.tensor_copy, 2, 0, J)
-        keys_gradient(2)
+        keys_gradient(1)
+        ds_cols[2] = keep.tile([P, J * C], BF16, name="ds_cols2", tag=TAGS[2], align_bytes=64)
+        pool_copy(ds_cols[2][:].rearrange("p (s j) -> p s j", j=J), ds_rows[2][:].rearrange("p j s -> p s j"))
+        place(nc.scalar.copy, 1)
         weigh(3, 0, J)
+        keys_gradient(2)
         weave_ds(nc.vector.tensor_copy, 3, 0, J)
-        place(nc.vector.tensor_copy, 2)
         keys_gradient(3)
+        place(nc.scalar.copy, 2)
         place(nc.vector.tensor_copy, 3)
         nc.sync.dma_start(out=out, in_=window[:])

@@ -7,6 +7,7 @@ FLOPS = 335544320
 F32 = mybir.dt.float32
 BF16 = mybir.dt.bfloat16
 U32 = mybir.dt.uint32
+I32 = mybir.dt.int32
 U16 = mybir.dt.uint16
 U8 = mybir.dt.uint8
 E4M3X4 = mybir.dt.float8_e4m3fn_x4
@@ -49,18 +50,15 @@ def tile_attend_bwd_kernel(tc, doT, vT, p, delta, qm, offs, out):
 
         offsets = keep.tile([P, N // 16], U16, name="offsets")
         do_rows = doT[0].rearrange("(p j) q -> p j q", j=J)
-        do_raw = []
-        for h in range(2):
-            t = keep.tile([P, J, QH], F32, name=f"do_raw{h}")
-            nc.sync.dma_start(out=t[:], in_=do_rows[:, :, h * QH : (h + 1) * QH])
-            do_raw.append(t)
-        nc.sync.dma_start(offsets[:], offs)
         v_rows = vT.rearrange("(p j) t -> p j t", j=J)
-        v_raw = []
-        for j in range(J):
-            t = keep.tile([P, T], F32, name=f"v_raw{j}")
-            nc.sync.dma_start(out=t[:], in_=v_rows[:, j, :])
-            v_raw.append(t)
+        do_raw = [keep.tile([P, J, QH], F32, name=f"do_raw{h}") for h in range(2)]
+        v_raw = [keep.tile([P, T], F32, name=f"v_raw{j}") for j in range(J)]
+        for h in range(2):
+            nc.sync.dma_start(out=do_raw[h][:], in_=do_rows[:, :, h * QH : (h + 1) * QH])
+            if h == 0:
+                nc.sync.dma_start(offsets[:], offs)
+            for j in ((0, 1), (2, 3))[h]:
+                nc.sync.dma_start(out=v_raw[j][:], in_=v_rows[:, j, :])
         qm_raw = keep.tile([P, J, D], F32, name="qm_raw")
         nc.sync.dma_start(out=qm_raw[:], in_=qm[0].rearrange("(p j) d -> p j d", j=J))
         delta_col = keep.tile([P, J], F32, name="delta_col")
@@ -89,14 +87,19 @@ def tile_attend_bwd_kernel(tc, doT, vT, p, delta, qm, offs, out):
                 do_raw[h][:].rearrange("p j (m t) -> p m j t", t=J)[:, :, :, t0:t1],
             )
 
-        weave_do(scalar_cast, 0, 0, J)
-        weave_do(nc.vector.tensor_copy, 1, 0, 2)
-        weave_do(scalar_cast, 1, 2, J)
-        for c0 in (0, QH):
-            cols = slice(c0, c0 + QH)
-            nc.vector.quantize_mx(
-                out=do_codes[:, cols].bitcast(E5M2X4), scales=do_scales[:, cols], in_=do_cols[:, J * c0 : J * (c0 + QH)]
-            )
+        def quantise_do(h):
+            for t in range(J):
+                c0 = t * P + h * (P // 2)
+                cols = slice(c0, c0 + P // 2)
+                nc.vector.quantize_mx(
+                    out=do_codes[:, cols].bitcast(E5M2X4),
+                    scales=do_scales[:, cols],
+                    in_=do_cols[:, J * c0 : J * (c0 + P // 2)],
+                )
+
+        weave_do(nc.vector.tensor_copy, 0, 0, 2)
+        weave_do(scalar_cast, 0, 2, J)
+        quantise_do(0)
 
         v_low = keep.tile([P, J * NV], BF16, name="v_low", align_bytes=64)
         v_lanes = v_low[:].rearrange("p (s j) -> p s j", j=J)
@@ -118,6 +121,9 @@ def tile_attend_bwd_kernel(tc, doT, vT, p, delta, qm, offs, out):
             nc.vector.tensor_copy(v_lanes[:, :, j], v_raw[j][:].indirect(listed(0, NV)))
             if j == 1:
                 weave(nc.scalar.copy, v_high[:], v_picked, 0, 2)
+                weave_do(nc.vector.tensor_copy, 1, 0, 2)
+                weave_do(nc.vector.tensor_copy, 1, 2, J)
+                quantise_do(1)
         for s0 in range(0, N - NV, C):
             nc.scalar.activation(
                 v_picked[:, J - 1, s0 : s0 + C], v_raw[J - 1][:].indirect(listed(NV + s0, NV + s0 + C)), ACT.Copy
@@ -160,15 +166,18 @@ def tile_attend_bwd_kernel(tc, doT, vT, p, delta, qm, offs, out):
             for t in range(J):
                 dp_pass(dp[c, t], c, t)
 
-        ds_rows = [keep.tile([P, J, C], BF16, name=f"ds_rows{c}") for c in range(J)]
+        ds_rows = [keep.tile([P, J, C], BF16, name=f"ds_rows{c}") for c in range(J - 1)]
+        ds_pairs = keep.tile([P, J * C], BF16, name="ds_pairs")
+        pair_lanes = ds_pairs[:].rearrange("p (u s e) -> p u e s", u=2, e=2)
         ds_cols = {}
         dk_cols = [keep.tile([P, C], F32, name=f"dk_cols{c}") for c in range(J)]
         dk = {}
 
         def weigh(c, t0, t1):
             for t in range(t0, t1):
+                dst = ds_rows[c][:, t, :] if c < J - 1 else pair_lanes[:, t // 2, t % 2, :]
                 nc.vector.scalar_tensor_tensor(
-                    ds_rows[c][:, t, :], dp[c, t], delta_col[:, t : t + 1], p_raw[c][:, t, :], ALU.subtract, ALU.mult
+                    dst, dp[c, t], delta_col[:, t : t + 1], p_raw[c][:, t, :], ALU.subtract, ALU.mult
                 )
 
         def pool_copy(dst, src):
@@ -219,7 +228,11 @@ def tile_attend_bwd_kernel(tc, doT, vT, p, delta, qm, offs, out):
         place(nc.scalar.copy, 1)
         weigh(3, 0, J)
         keys_gradient(2)
-        weave_ds(nc.vector.tensor_copy, 3, 0, J)
+        ds_cols[3] = keep.tile([P, J * C], BF16, name="ds_cols3", align_bytes=64)
+        nc.vector.tensor_copy(
+            ds_cols[3][:].bitcast(I32).rearrange("p (c i u) -> p c u i", i=4, u=2),
+            ds_pairs[:].bitcast(I32).rearrange("p (u c i) -> p c u i", i=4, u=2),
+        )
         keys_gradient(3)
         place(nc.scalar.copy, 2)
         place(nc.vector.tensor_copy, 3)

@@ -7,7 +7,6 @@ FLOPS = 335544320
 F32 = mybir.dt.float32
 BF16 = mybir.dt.bfloat16
 U32 = mybir.dt.uint32
-I32 = mybir.dt.int32
 U16 = mybir.dt.uint16
 U8 = mybir.dt.uint8
 E4M3X4 = mybir.dt.float8_e4m3fn_x4
@@ -48,17 +47,24 @@ def tile_attend_bwd_kernel(tc, doT, vT, p, delta, qm, offs, out):
         def scalar_cast(dst, src):
             nc.scalar.activation(dst, src, ACT.Copy)
 
+        def pool_weave(dst, src):
+            nc.gpsimd.tensor_scalar(
+                dst.rearrange("p (s j) -> p s j", j=J), src.rearrange("p j s -> p s j"), 1.0, 0.0, ALU.mult, ALU.add
+            )
+
         offsets = keep.tile([P, N // 16], U16, name="offsets")
         do_rows = doT[0].rearrange("(p j) q -> p j q", j=J)
         v_rows = vT.rearrange("(p j) t -> p j t", j=J)
-        do_raw = [keep.tile([P, J, QH], F32, name=f"do_raw{h}") for h in range(2)]
+        do_raw = [
+            keep.tile([P, J, QH], F32, name="do_first"),
+            reused.tile([P, J, QH], F32, name="do_second", align_bytes=64, offset=0),
+        ]
         v_raw = [keep.tile([P, T], F32, name=f"v_raw{j}") for j in range(J)]
-        for h in range(2):
-            nc.sync.dma_start(out=do_raw[h][:], in_=do_rows[:, :, h * QH : (h + 1) * QH])
-            if h == 0:
-                nc.sync.dma_start(offsets[:], offs)
-            for j in ((0, 1), (2, 3))[h]:
-                nc.sync.dma_start(out=v_raw[j][:], in_=v_rows[:, j, :])
+        nc.sync.dma_start(out=do_raw[0][:], in_=do_rows[:, :, 0:QH])
+        nc.sync.dma_start(offsets[:], offs)
+        for j in range(J):
+            nc.sync.dma_start(out=v_raw[j][:], in_=v_rows[:, j, :])
+        nc.sync.dma_start(out=do_raw[1][:], in_=do_rows[:, :, QH:Q])
         qm_raw = keep.tile([P, J, D], F32, name="qm_raw")
         nc.sync.dma_start(out=qm_raw[:], in_=qm[0].rearrange("(p j) d -> p j d", j=J))
         delta_col = keep.tile([P, J], F32, name="delta_col")
@@ -66,10 +72,7 @@ def tile_attend_bwd_kernel(tc, doT, vT, p, delta, qm, offs, out):
         p_rows = p[0].rearrange("(p j) s -> p j s", j=J)
         p_raw = []
         for s0, s1 in ((0, C), (C, 2 * C), (2 * C, N)):
-            if s0 == 0:
-                t = reused.tile([P, J, C], F32, name="p_first", align_bytes=64, offset=0)
-            else:
-                t = keep.tile([P, J, s1 - s0], F32, name=f"p_raw{s0}")
+            t = keep.tile([P, J, s1 - s0], F32, name=f"p_raw{s0}")
             nc.sync.dma_start(out=t[:], in_=p_rows[:, :, s0:s1])
             for c0 in range(0, s1 - s0, C):
                 p_raw.append(t[:, :, c0 : c0 + C])
@@ -77,67 +80,64 @@ def tile_attend_bwd_kernel(tc, doT, vT, p, delta, qm, offs, out):
         window = keep.tile([P, T], F32, name="window")
         nc.gpsimd.memset(window[:], 0.0)
 
-        do_cols = keep.tile([P, J * Q], BF16, name="do_cols", align_bytes=64)
+        do_cols = [keep.tile([P, J * QH], BF16, name=f"do_cols{u}", align_bytes=64) for u in range(2)]
         do_codes = keep.tile([P, Q], U32, name="do_codes", align_bytes=64)
         do_scales = keep.tile([P, Q], U8, name="do_scales", align_bytes=64)
 
         def weave_do(engine_copy, h, t0, t1):
             engine_copy(
-                do_cols[:].rearrange("p (t h m j) -> p h m j t", t=J, h=2, j=J)[:, h, :, :, t0:t1],
+                do_cols[t0 // 2][:].rearrange("p (t h m j) -> p h m j t", t=2, h=2, j=J)[:, h, :, :, :],
                 do_raw[h][:].rearrange("p j (m t) -> p m j t", t=J)[:, :, :, t0:t1],
             )
 
-        def quantise_do(h):
-            for t in range(J):
+        def quantise_do(h, t0, t1):
+            for t in range(t0, t1):
                 c0 = t * P + h * (P // 2)
                 cols = slice(c0, c0 + P // 2)
                 nc.vector.quantize_mx(
                     out=do_codes[:, cols].bitcast(E5M2X4),
                     scales=do_scales[:, cols],
-                    in_=do_cols[:, J * c0 : J * (c0 + P // 2)],
+                    in_=do_cols[t // 2][:, J * (c0 % QH) : J * (c0 % QH + P // 2)],
                 )
-
-        weave_do(nc.vector.tensor_copy, 0, 0, 2)
-        weave_do(scalar_cast, 0, 2, J)
-        quantise_do(0)
 
         v_low = keep.tile([P, J * NV], BF16, name="v_low", align_bytes=64)
         v_lanes = v_low[:].rearrange("p (s j) -> p s j", j=J)
-        v_high = keep.tile([P, J * (N - NV)], BF16, name="v_high", align_bytes=64)
+        v_third = keep.tile([P, J * C], BF16, name="v_third", align_bytes=64)
         v_picked = keep.tile([P, J, N - NV], BF16, name="v_picked")
         v_codes = {}
         v_scales = keep.tile([P, N], U8, name="v_scales", align_bytes=64)
 
         def quantise_v(s0, s1, src):
-            if s1 == N:
-                codes = reused.tile([P, C], U32, name="v_codes_last", align_bytes=64, offset=0)
+            if s0 == NV:
+                codes = reused.tile([P, C], U32, name="v_codes_third", align_bytes=64, offset=0)
             else:
                 codes = keep.tile([P, C], U32, name=f"v_codes{s0}", align_bytes=64)
             v_codes[s0 // C] = codes
             nc.vector.quantize_mx(out=codes[:].bitcast(E4M3X4), scales=v_scales[:, s0:s1], in_=src)
 
-        for j in range(J - 1):
-            nc.scalar.activation(v_picked[:, j, :], v_raw[j][:].indirect(listed(NV, N)), ACT.Copy)
-            nc.vector.tensor_copy(v_lanes[:, :, j], v_raw[j][:].indirect(listed(0, NV)))
-            if j == 1:
-                weave(nc.scalar.copy, v_high[:], v_picked, 0, 2)
-                weave_do(nc.vector.tensor_copy, 1, 0, 2)
-                weave_do(nc.vector.tensor_copy, 1, 2, J)
-                quantise_do(1)
-        for s0 in range(0, N - NV, C):
-            nc.scalar.activation(
-                v_picked[:, J - 1, s0 : s0 + C], v_raw[J - 1][:].indirect(listed(NV + s0, NV + s0 + C)), ACT.Copy
-            )
-            weave(nc.scalar.copy, v_high[:, J * s0 : J * (s0 + C)], v_picked[:, :, s0 : s0 + C], 2, J)
-        for s0 in range(0, NV, C):
-            nc.vector.tensor_copy(v_lanes[:, s0 : s0 + C, J - 1], v_raw[J - 1][:].indirect(listed(s0, s0 + C)))
-            quantise_v(s0, s0 + C, v_low[:, J * s0 : J * (s0 + C)])
+        weave_do(nc.vector.tensor_copy, 0, 0, 2)
+        weave_do(scalar_cast, 0, 2, J)
+        quantise_do(0, 0, J)
+        for j in range(J):
+            for s0, s1 in ((NV, N),) if j < J - 1 else ((NV, NV + C), (NV + C, N)):
+                nc.scalar.activation(v_picked[:, j, s0 - NV : s1 - NV], v_raw[j][:].indirect(listed(s0, s1)), ACT.Copy)
+            for s0, s1 in ((0, NV),) if j < J - 1 else ((0, C), (C, NV)):
+                nc.vector.tensor_copy(v_lanes[:, s0:s1, j], v_raw[j][:].indirect(listed(s0, s1)))
+            if j % 2 == 1:
+                weave(nc.scalar.copy, v_third[:], v_picked[:, :, 0:C], j - 1, j + 1)
+        quantise_v(0, C, v_low[:, 0 : J * C])
+        quantise_v(C, NV, v_low[:, J * C : J * NV])
+        weave_do(nc.vector.tensor_copy, 1, 0, 2)
+        weave_do(nc.scalar.copy, 1, 2, J)
+        quantise_do(1, 0, J)
+        quantise_v(NV, NV + C, v_third[:])
 
-        quantise_v(2 * C, 3 * C, v_high[:, 0 : J * C])
         qm_cols = keep.tile([P, J * D], BF16, name="qm_cols", align_bytes=64)
-        qm_codes = reused.tile([P, D], U32, name="qm_codes", align_bytes=64, offset=4 * C)
+        qm_codes = keep.tile([P, D], U32, name="qm_codes", align_bytes=64)
         qm_scales = keep.tile([P, D], U8, name="qm_scales", align_bytes=64)
-        weave(nc.vector.tensor_copy, qm_cols[:], qm_raw, 0, J)
+        weave(nc.scalar.copy, qm_cols[:], qm_raw, 0, J)
+        v_last = reused.tile([P, J * C], BF16, name="v_last", align_bytes=64, offset=4 * C)
+        weave(nc.scalar.copy, v_last[:], v_picked[:, :, C : 2 * C], 0, J)
 
         def dp_pass(dst, c, t):
             cols = slice(t * P, (t + 1) * P)
@@ -166,22 +166,16 @@ def tile_attend_bwd_kernel(tc, doT, vT, p, delta, qm, offs, out):
             for t in range(J):
                 dp_pass(dp[c, t], c, t)
 
-        ds_rows = [keep.tile([P, J, C], BF16, name=f"ds_rows{c}") for c in range(J - 1)]
-        ds_pairs = keep.tile([P, J * C], BF16, name="ds_pairs")
-        pair_lanes = ds_pairs[:].rearrange("p (u s e) -> p u e s", u=2, e=2)
+        ds_rows = [keep.tile([P, J, C], BF16, name=f"ds_rows{c}") for c in range(J)]
         ds_cols = {}
         dk_cols = [keep.tile([P, C], F32, name=f"dk_cols{c}") for c in range(J)]
         dk = {}
 
         def weigh(c, t0, t1):
             for t in range(t0, t1):
-                dst = ds_rows[c][:, t, :] if c < J - 1 else pair_lanes[:, t // 2, t % 2, :]
                 nc.vector.scalar_tensor_tensor(
-                    dst, dp[c, t], delta_col[:, t : t + 1], p_raw[c][:, t, :], ALU.subtract, ALU.mult
+                    ds_rows[c][:, t, :], dp[c, t], delta_col[:, t : t + 1], p_raw[c][:, t, :], ALU.subtract, ALU.mult
                 )
-
-        def pool_copy(dst, src):
-            nc.gpsimd.tensor_scalar(dst, src, 1.0, 0.0, ALU.mult, ALU.add)
 
         def weave_ds(engine_copy, c, j0, j1):
             if j0 == 0:
@@ -219,20 +213,16 @@ def tile_attend_bwd_kernel(tc, doT, vT, p, delta, qm, offs, out):
         nc.vector.quantize_mx(out=qm_codes[:].bitcast(E4M3X4), scales=qm_scales[:], in_=qm_cols[:])
         keys_gradient(0)
         place(nc.scalar.copy, 0)
-        quantise_v(3 * C, N, v_high[:, J * C : 2 * J * C])
+        quantise_v(3 * C, N, v_last[:])
         scores_gradient(3)
         weigh(2, 0, J)
         keys_gradient(1)
         ds_cols[2] = keep.tile([P, J * C], BF16, name="ds_cols2", tag=TAGS[2], align_bytes=64)
-        pool_copy(ds_cols[2][:].rearrange("p (s j) -> p s j", j=J), ds_rows[2][:].rearrange("p j s -> p s j"))
+        pool_weave(ds_cols[2][:], ds_rows[2][:])
         place(nc.scalar.copy, 1)
         weigh(3, 0, J)
         keys_gradient(2)
-        ds_cols[3] = keep.tile([P, J * C], BF16, name="ds_cols3", align_bytes=64)
-        nc.vector.tensor_copy(
-            ds_cols[3][:].bitcast(I32).rearrange("p (c i u) -> p c u i", i=4, u=2),
-            ds_pairs[:].bitcast(I32).rearrange("p (u c i) -> p c u i", i=4, u=2),
-        )
+        weave_ds(nc.vector.tensor_copy, 3, 0, J)
         keys_gradient(3)
         place(nc.scalar.copy, 2)
         place(nc.vector.tensor_copy, 3)

@@ -55,10 +55,7 @@ def tile_attend_bwd_kernel(tc, doT, vT, p, delta, qm, offs, out):
         offsets = keep.tile([P, N // 16], U16, name="offsets")
         do_rows = doT[0].rearrange("(p j) q -> p j q", j=J)
         v_rows = vT.rearrange("(p j) t -> p j t", j=J)
-        do_raw = [
-            keep.tile([P, J, QH], F32, name="do_first"),
-            reused.tile([P, J, QH], F32, name="do_second", align_bytes=64, offset=0),
-        ]
+        do_raw = [keep.tile([P, J, QH], F32, name=f"do_raw{h}") for h in range(2)]
         v_raw = [keep.tile([P, T], F32, name=f"v_raw{j}") for j in range(J)]
         nc.sync.dma_start(out=do_raw[0][:], in_=do_rows[:, :, 0:QH])
         nc.sync.dma_start(offsets[:], offs)
@@ -80,7 +77,10 @@ def tile_attend_bwd_kernel(tc, doT, vT, p, delta, qm, offs, out):
         window = keep.tile([P, T], F32, name="window")
         nc.gpsimd.memset(window[:], 0.0)
 
-        do_cols = [keep.tile([P, J * QH], BF16, name=f"do_cols{u}", align_bytes=64) for u in range(2)]
+        do_cols = [
+            keep.tile([P, J * QH], BF16, name="do_cols_low", align_bytes=64),
+            reused.tile([P, J * QH], BF16, name="do_cols_high", align_bytes=64, offset=0),
+        ]
         do_codes = keep.tile([P, Q], U32, name="do_codes", align_bytes=64)
         do_scales = keep.tile([P, Q], U8, name="do_scales", align_bytes=64)
 
@@ -108,8 +108,8 @@ def tile_attend_bwd_kernel(tc, doT, vT, p, delta, qm, offs, out):
         v_scales = keep.tile([P, N], U8, name="v_scales", align_bytes=64)
 
         def quantise_v(s0, s1, src):
-            if s0 == NV:
-                codes = reused.tile([P, C], U32, name="v_codes_third", align_bytes=64, offset=0)
+            if s0 in (C, 2 * C):
+                codes = reused.tile([P, C], U32, name=f"v_codes{s0}", align_bytes=64, offset=4 * (s0 - C))
             else:
                 codes = keep.tile([P, C], U32, name=f"v_codes{s0}", align_bytes=64)
             v_codes[s0 // C] = codes
@@ -126,18 +126,19 @@ def tile_attend_bwd_kernel(tc, doT, vT, p, delta, qm, offs, out):
             if j % 2 == 1:
                 weave(nc.scalar.copy, v_third[:], v_picked[:, :, 0:C], j - 1, j + 1)
         quantise_v(0, C, v_low[:, 0 : J * C])
-        quantise_v(C, NV, v_low[:, J * C : J * NV])
         weave_do(nc.vector.tensor_copy, 1, 0, 2)
         weave_do(nc.scalar.copy, 1, 2, J)
         quantise_do(1, 0, J)
+        quantise_v(C, NV, v_low[:, J * C : J * NV])
         quantise_v(NV, NV + C, v_third[:])
 
         qm_cols = keep.tile([P, J * D], BF16, name="qm_cols", align_bytes=64)
         qm_codes = keep.tile([P, D], U32, name="qm_codes", align_bytes=64)
         qm_scales = keep.tile([P, D], U8, name="qm_scales", align_bytes=64)
         weave(nc.scalar.copy, qm_cols[:], qm_raw, 0, J)
-        v_last = reused.tile([P, J * C], BF16, name="v_last", align_bytes=64, offset=4 * C)
-        weave(nc.scalar.copy, v_last[:], v_picked[:, :, C : 2 * C], 0, J)
+        nc.vector.quantize_mx(out=qm_codes[:].bitcast(E4M3X4), scales=qm_scales[:], in_=qm_cols[:])
+        v_last = qm_cols
+        pool_weave(v_last[:], v_picked[:, :, C : 2 * C])
 
         def dp_pass(dst, c, t):
             cols = slice(t * P, (t + 1) * P)
@@ -210,7 +211,6 @@ def tile_attend_bwd_kernel(tc, doT, vT, p, delta, qm, offs, out):
             weave_ds(nc.scalar.copy, c, 0, 2)
             weigh(c, 2, J)
             weave_ds(nc.scalar.copy, c, 2, J)
-        nc.vector.quantize_mx(out=qm_codes[:].bitcast(E4M3X4), scales=qm_scales[:], in_=qm_cols[:])
         keys_gradient(0)
         place(nc.scalar.copy, 0)
         quantise_v(3 * C, N, v_last[:])
@@ -219,11 +219,11 @@ def tile_attend_bwd_kernel(tc, doT, vT, p, delta, qm, offs, out):
         keys_gradient(1)
         ds_cols[2] = keep.tile([P, J * C], BF16, name="ds_cols2", tag=TAGS[2], align_bytes=64)
         pool_weave(ds_cols[2][:], ds_rows[2][:])
-        place(nc.scalar.copy, 1)
+        place(nc.vector.tensor_copy, 1)
         weigh(3, 0, J)
         keys_gradient(2)
         weave_ds(nc.vector.tensor_copy, 3, 0, J)
+        place(nc.vector.tensor_copy, 2)
         keys_gradient(3)
-        place(nc.scalar.copy, 2)
         place(nc.vector.tensor_copy, 3)
         nc.sync.dma_start(out=out, in_=window[:])

@@ -55,7 +55,7 @@ def tile_attend_bwd_kernel(tc, doT, vT, p, delta, qm, offs, out):
         offsets = keep.tile([P, N // 16], U16, name="offsets")
         do_rows = doT[0].rearrange("(p j) q -> p j q", j=J)
         v_rows = vT.rearrange("(p j) t -> p j t", j=J)
-        do_raw = [keep.tile([P, J, QH], F32, name=f"do_raw{h}") for h in range(2)]
+        do_raw = [keep.tile([P, J, QH], F32, name=f"do_raw{h}", tag=f"do_raw{h}", align_bytes=64) for h in range(2)]
         v_raw = [keep.tile([P, T], F32, name=f"v_raw{j}") for j in range(J)]
         nc.sync.dma_start(out=do_raw[0][:], in_=do_rows[:, :, 0:QH])
         nc.sync.dma_start(offsets[:], offs)
@@ -102,14 +102,13 @@ def tile_attend_bwd_kernel(tc, doT, vT, p, delta, qm, offs, out):
 
         v_low = keep.tile([P, J * NV], BF16, name="v_low", align_bytes=64)
         v_lanes = v_low[:].rearrange("p (s j) -> p s j", j=J)
-        v_third = keep.tile([P, J * C], BF16, name="v_third", align_bytes=64)
         v_picked = keep.tile([P, J, N - NV], BF16, name="v_picked")
         v_codes = {}
         v_scales = keep.tile([P, N], U8, name="v_scales", align_bytes=64)
 
         def quantise_v(s0, s1, src):
-            if s0 in (C, 2 * C):
-                codes = reused.tile([P, C], U32, name=f"v_codes{s0}", align_bytes=64, offset=4 * (s0 - C))
+            if s0 == C:
+                codes = reused.tile([P, C], U32, name=f"v_codes{s0}", align_bytes=64, offset=0)
             else:
                 codes = keep.tile([P, C], U32, name=f"v_codes{s0}", align_bytes=64)
             v_codes[s0 // C] = codes
@@ -119,24 +118,22 @@ def tile_attend_bwd_kernel(tc, doT, vT, p, delta, qm, offs, out):
         weave_do(scalar_cast, 0, 2, J)
         quantise_do(0, 0, J)
         for j in range(J):
-            for s0, s1 in ((NV, N),) if j < J - 1 else ((NV, NV + C), (NV + C, N)):
-                nc.scalar.activation(v_picked[:, j, s0 - NV : s1 - NV], v_raw[j][:].indirect(listed(s0, s1)), ACT.Copy)
+            nc.scalar.activation(v_picked[:, j, :], v_raw[j][:].indirect(listed(NV, N)), ACT.Copy)
             for s0, s1 in ((0, NV),) if j < J - 1 else ((0, C), (C, NV)):
                 nc.vector.tensor_copy(v_lanes[:, s0:s1, j], v_raw[j][:].indirect(listed(s0, s1)))
-            if j % 2 == 1:
-                weave(nc.scalar.copy, v_third[:], v_picked[:, :, 0:C], j - 1, j + 1)
         quantise_v(0, C, v_low[:, 0 : J * C])
         weave_do(nc.vector.tensor_copy, 1, 0, 2)
         weave_do(nc.scalar.copy, 1, 2, J)
         quantise_do(1, 0, J)
         quantise_v(C, NV, v_low[:, J * C : J * NV])
-        quantise_v(NV, NV + C, v_third[:])
 
         qm_cols = keep.tile([P, J * D], BF16, name="qm_cols", align_bytes=64)
         qm_codes = keep.tile([P, D], U32, name="qm_codes", align_bytes=64)
         qm_scales = keep.tile([P, D], U8, name="qm_scales", align_bytes=64)
         weave(nc.scalar.copy, qm_cols[:], qm_raw, 0, J)
         nc.vector.quantize_mx(out=qm_codes[:].bitcast(E4M3X4), scales=qm_scales[:], in_=qm_cols[:])
+        v_third = keep.tile([P, J * C], BF16, name="v_third", tag="do_raw1", align_bytes=64)
+        weave(nc.scalar.copy, v_third[:], v_picked[:, :, 0:C], 0, J)
         v_last = qm_cols
         pool_weave(v_last[:], v_picked[:, :, C : 2 * C])
 
@@ -205,12 +202,16 @@ def tile_attend_bwd_kernel(tc, doT, vT, p, delta, qm, offs, out):
 
         scores_gradient(0)
         scores_gradient(1)
+        weigh(0, 0, 2)
+        weave_ds(nc.scalar.copy, 0, 0, 2)
+        weigh(0, 2, J)
+        weave_ds(nc.scalar.copy, 0, 2, J)
+        weigh(1, 0, 2)
+        weave_ds(nc.scalar.copy, 1, 0, 2)
+        quantise_v(2 * C, 3 * C, v_third[:])
         scores_gradient(2)
-        for c in range(2):
-            weigh(c, 0, 2)
-            weave_ds(nc.scalar.copy, c, 0, 2)
-            weigh(c, 2, J)
-            weave_ds(nc.scalar.copy, c, 2, J)
+        weigh(1, 2, J)
+        weave_ds(nc.scalar.copy, 1, 2, J)
         keys_gradient(0)
         place(nc.scalar.copy, 0)
         quantise_v(3 * C, N, v_last[:])
@@ -219,11 +220,11 @@ def tile_attend_bwd_kernel(tc, doT, vT, p, delta, qm, offs, out):
         keys_gradient(1)
         ds_cols[2] = keep.tile([P, J * C], BF16, name="ds_cols2", tag=TAGS[2], align_bytes=64)
         pool_weave(ds_cols[2][:], ds_rows[2][:])
-        place(nc.vector.tensor_copy, 1)
+        place(nc.scalar.copy, 1)
         weigh(3, 0, J)
         keys_gradient(2)
         weave_ds(nc.vector.tensor_copy, 3, 0, J)
-        place(nc.vector.tensor_copy, 2)
         keys_gradient(3)
+        place(nc.scalar.copy, 2)
         place(nc.vector.tensor_copy, 3)
         nc.sync.dma_start(out=out, in_=window[:])

@@ -25,6 +25,7 @@ QH = Q // 2
 WEAVE_OUT = "p (c i j) -> p c j i"
 WEAVE_IN = "p j (c i) -> p c j i"
 NV = 256
+P_FIRST = 2 * J * QH
 TAGS = ("ds_a", "ds_b", "ds_b", "ds_d")
 
 
@@ -69,7 +70,10 @@ def tile_attend_bwd_kernel(tc, doT, vT, p, delta, qm, offs, out):
         p_rows = p[0].rearrange("(p j) s -> p j s", j=J)
         p_raw = []
         for s0, s1 in ((0, C), (C, 2 * C), (2 * C, N)):
-            t = keep.tile([P, J, s1 - s0], F32, name=f"p_raw{s0}")
+            if s0 == 0:
+                t = reused.tile([P, J, C], F32, name="p_first", align_bytes=64, offset=P_FIRST)
+            else:
+                t = keep.tile([P, J, s1 - s0], F32, name=f"p_raw{s0}")
             nc.sync.dma_start(out=t[:], in_=p_rows[:, :, s0:s1])
             for c0 in range(0, s1 - s0, C):
                 p_raw.append(t[:, :, c0 : c0 + C])
@@ -109,6 +113,8 @@ def tile_attend_bwd_kernel(tc, doT, vT, p, delta, qm, offs, out):
         def quantise_v(s0, s1, src):
             if s0 == C:
                 codes = reused.tile([P, C], U32, name=f"v_codes{s0}", align_bytes=64, offset=0)
+            elif s0 == 2 * C:
+                codes = reused.tile([P, C], U32, name=f"v_codes{s0}", align_bytes=64, offset=P_FIRST + 4 * D)
             else:
                 codes = keep.tile([P, C], U32, name=f"v_codes{s0}", align_bytes=64)
             v_codes[s0 // C] = codes
@@ -128,14 +134,13 @@ def tile_attend_bwd_kernel(tc, doT, vT, p, delta, qm, offs, out):
         quantise_v(C, NV, v_low[:, J * C : J * NV])
 
         qm_cols = keep.tile([P, J * D], BF16, name="qm_cols", align_bytes=64)
-        qm_codes = keep.tile([P, D], U32, name="qm_codes", align_bytes=64)
         qm_scales = keep.tile([P, D], U8, name="qm_scales", align_bytes=64)
         weave(nc.scalar.copy, qm_cols[:], qm_raw, 0, J)
-        nc.vector.quantize_mx(out=qm_codes[:].bitcast(E4M3X4), scales=qm_scales[:], in_=qm_cols[:])
         v_third = keep.tile([P, J * C], BF16, name="v_third", tag="do_raw1", align_bytes=64)
         weave(nc.scalar.copy, v_third[:], v_picked[:, :, 0:C], 0, J)
-        v_last = qm_cols
-        pool_weave(v_last[:], v_picked[:, :, C : 2 * C])
+        v_last = v_low[:, J * C : J * NV]
+        pool_weave(v_last, v_picked[:, :, C : 2 * C])
+        qm_codes = reused.tile([P, D], U32, name="qm_codes", align_bytes=64, offset=P_FIRST)
 
         def dp_pass(dst, c, t):
             cols = slice(t * P, (t + 1) * P)
@@ -152,16 +157,10 @@ def tile_attend_bwd_kernel(tc, doT, vT, p, delta, qm, offs, out):
 
         dp = {}
 
-        def scores_gradient(c):
-            if c == 0:
-                for t in range(J):
-                    bank = psum.tile([P, C], F32, name=f"first{t}", tag=f"bank{t}")
-                    dp[c, t] = bank[:]
-            else:
-                bank = psum.tile([P, J, C], F32, name=f"dp{c}", tag=f"bank{J - 1 + c}")
-                for t in range(J):
-                    dp[c, t] = bank[:, t, :]
-            for t in range(J):
+        def scores_gradient(c, t0, t1, bank_name):
+            bank = psum.tile([P, t1 - t0, C], F32, name=f"dp{c}_{t0}", tag=bank_name)
+            for t in range(t0, t1):
+                dp[c, t] = bank[:, t - t0, :]
                 dp_pass(dp[c, t], c, t)
 
         ds_rows = [keep.tile([P, J, C], BF16, name=f"ds_rows{c}") for c in range(J)]
@@ -184,7 +183,7 @@ def tile_attend_bwd_kernel(tc, doT, vT, p, delta, qm, offs, out):
             codes = keep.tile([P, C], U32, name=f"ds_codes{c}", align_bytes=64)
             scales = keep.tile([P, C], U8, name=f"ds_scales{c}", align_bytes=64)
             nc.vector.quantize_mx(out=codes[:].bitcast(E5M2X4), scales=scales[:], in_=ds_cols[c][:])
-            bank = psum.tile([P, C], F32, name=f"dk{c}", tag=f"bank{(c + 7) % 8}")
+            bank = psum.tile([P, C], F32, name=f"dk{c}", tag=("bank7", "bank2", "bank4", "bank5")[c])
             nc.tensor.matmul_mx(
                 out=bank[:],
                 lhsT=qm_codes[:].bitcast(E4M3X4),
@@ -200,22 +199,28 @@ def tile_attend_bwd_kernel(tc, doT, vT, p, delta, qm, offs, out):
             engine_copy(dk_cols[c][:], dk[c][:])
             nc.scalar.activation(window[:].indirect(listed(c * C, (c + 1) * C)), dk_cols[c][:], ACT.Copy)
 
-        scores_gradient(0)
-        scores_gradient(1)
+        for t in range(J):
+            scores_gradient(0, t, t + 1, f"bank{t}")
+        scores_gradient(1, 0, 2, "bank4")
+        scores_gradient(1, 2, J, "bank5")
         weigh(0, 0, 2)
         weave_ds(nc.scalar.copy, 0, 0, 2)
         weigh(0, 2, J)
         weave_ds(nc.scalar.copy, 0, 2, J)
-        weigh(1, 0, 2)
-        weave_ds(nc.scalar.copy, 1, 0, 2)
+        weigh(1, 0, 1)
         quantise_v(2 * C, 3 * C, v_third[:])
-        scores_gradient(2)
+        scores_gradient(2, 0, 2, "bank6")
+        scores_gradient(2, 2, J, "bank3")
+        weigh(1, 1, 2)
+        weave_ds(nc.scalar.copy, 1, 0, 2)
         weigh(1, 2, J)
         weave_ds(nc.scalar.copy, 1, 2, J)
+        nc.vector.quantize_mx(out=qm_codes[:].bitcast(E4M3X4), scales=qm_scales[:], in_=qm_cols[:])
         keys_gradient(0)
         place(nc.scalar.copy, 0)
-        quantise_v(3 * C, N, v_last[:])
-        scores_gradient(3)
+        quantise_v(3 * C, N, v_last)
+        scores_gradient(3, 0, 2, "bank0")
+        scores_gradient(3, 2, J, "bank1")
         weigh(2, 0, J)
         keys_gradient(1)
         ds_cols[2] = keep.tile([P, J * C], BF16, name="ds_cols2", tag=TAGS[2], align_bytes=64)

@@ -26,6 +26,8 @@ WEAVE_OUT = "p (c i j) -> p c j i"
 WEAVE_IN = "p j (c i) -> p c j i"
 NV = 256
 P_FIRST = 2 * J * QH
+DO_SECOND = P_FIRST + 4 * J * C
+MH = QH // J
 TAGS = ("ds_a", "ds_b", "ds_b", "ds_d")
 
 
@@ -56,7 +58,10 @@ def tile_attend_bwd_kernel(tc, doT, vT, p, delta, qm, offs, out):
         offsets = keep.tile([P, N // 16], U16, name="offsets")
         do_rows = doT[0].rearrange("(p j) q -> p j q", j=J)
         v_rows = vT.rearrange("(p j) t -> p j t", j=J)
-        do_raw = [keep.tile([P, J, QH], F32, name=f"do_raw{h}", tag=f"do_raw{h}", align_bytes=64) for h in range(2)]
+        do_raw = [
+            keep.tile([P, J, QH], F32, name="do_first"),
+            reused.tile([P, J, QH], F32, name="do_second", align_bytes=64, offset=DO_SECOND),
+        ]
         v_raw = [keep.tile([P, T], F32, name=f"v_raw{j}") for j in range(J)]
         nc.sync.dma_start(out=do_raw[0][:], in_=do_rows[:, :, 0:QH])
         nc.sync.dma_start(offsets[:], offs)
@@ -88,10 +93,10 @@ def tile_attend_bwd_kernel(tc, doT, vT, p, delta, qm, offs, out):
         do_codes = keep.tile([P, Q], U32, name="do_codes", align_bytes=64)
         do_scales = keep.tile([P, Q], U8, name="do_scales", align_bytes=64)
 
-        def weave_do(engine_copy, h, t0, t1):
+        def weave_do(engine_copy, h, t0, t1, m0=0, m1=MH):
             engine_copy(
-                do_cols[t0 // 2][:].rearrange("p (t h m j) -> p h m j t", t=2, h=2, j=J)[:, h, :, :, :],
-                do_raw[h][:].rearrange("p j (m t) -> p m j t", t=J)[:, :, :, t0:t1],
+                do_cols[t0 // 2][:].rearrange("p (t h m j) -> p h m j t", t=2, h=2, j=J)[:, h, m0:m1, :, :],
+                do_raw[h][:].rearrange("p j (m t) -> p m j t", t=J)[:, m0:m1, :, t0:t1],
             )
 
         def quantise_do(h, t0, t1):
@@ -114,7 +119,7 @@ def tile_attend_bwd_kernel(tc, doT, vT, p, delta, qm, offs, out):
             if s0 == C:
                 codes = reused.tile([P, C], U32, name=f"v_codes{s0}", align_bytes=64, offset=0)
             elif s0 == 2 * C:
-                codes = reused.tile([P, C], U32, name=f"v_codes{s0}", align_bytes=64, offset=P_FIRST + 4 * D)
+                codes = reused.tile([P, C], U32, name=f"v_codes{s0}", align_bytes=64, offset=DO_SECOND)
             else:
                 codes = keep.tile([P, C], U32, name=f"v_codes{s0}", align_bytes=64)
             v_codes[s0 // C] = codes
@@ -124,22 +129,25 @@ def tile_attend_bwd_kernel(tc, doT, vT, p, delta, qm, offs, out):
         weave_do(scalar_cast, 0, 2, J)
         quantise_do(0, 0, J)
         for j in range(J):
-            nc.scalar.activation(v_picked[:, j, :], v_raw[j][:].indirect(listed(NV, N)), ACT.Copy)
+            for s0, s1 in ((NV, N),) if j < J - 1 else ((NV, NV + C), (NV + C, N)):
+                nc.scalar.activation(v_picked[:, j, s0 - NV : s1 - NV], v_raw[j][:].indirect(listed(s0, s1)), ACT.Copy)
             for s0, s1 in ((0, NV),) if j < J - 1 else ((0, C), (C, NV)):
                 nc.vector.tensor_copy(v_lanes[:, s0:s1, j], v_raw[j][:].indirect(listed(s0, s1)))
+        v_third = keep.tile([P, J * C], BF16, name="v_third", align_bytes=64)
+        weave(nc.scalar.copy, v_third[:], v_picked[:, :, 0:C], 0, J)
         quantise_v(0, C, v_low[:, 0 : J * C])
         weave_do(nc.vector.tensor_copy, 1, 0, 2)
-        weave_do(nc.scalar.copy, 1, 2, J)
+        weave_do(nc.vector.tensor_copy, 1, 2, J, 0, MH // 2)
+        weave_do(nc.scalar.copy, 1, 2, J, MH // 2, MH)
         quantise_do(1, 0, J)
         quantise_v(C, NV, v_low[:, J * C : J * NV])
+        quantise_v(NV, NV + C, v_third[:])
 
         qm_cols = keep.tile([P, J * D], BF16, name="qm_cols", align_bytes=64)
         qm_scales = keep.tile([P, D], U8, name="qm_scales", align_bytes=64)
         weave(nc.scalar.copy, qm_cols[:], qm_raw, 0, J)
-        v_third = keep.tile([P, J * C], BF16, name="v_third", tag="do_raw1", align_bytes=64)
-        weave(nc.scalar.copy, v_third[:], v_picked[:, :, 0:C], 0, J)
-        v_last = v_low[:, J * C : J * NV]
-        pool_weave(v_last, v_picked[:, :, C : 2 * C])
+        v_last = reused.tile([P, J * C], BF16, name="v_last", align_bytes=64, offset=DO_SECOND + 4 * C)
+        weave(nc.scalar.copy, v_last[:], v_picked[:, :, C : 2 * C], 0, J)
         qm_codes = reused.tile([P, D], U32, name="qm_codes", align_bytes=64, offset=P_FIRST)
 
         def dp_pass(dst, c, t):
@@ -207,18 +215,16 @@ def tile_attend_bwd_kernel(tc, doT, vT, p, delta, qm, offs, out):
         weave_ds(nc.scalar.copy, 0, 0, 2)
         weigh(0, 2, J)
         weave_ds(nc.scalar.copy, 0, 2, J)
-        weigh(1, 0, 1)
-        quantise_v(2 * C, 3 * C, v_third[:])
         scores_gradient(2, 0, 2, "bank6")
         scores_gradient(2, 2, J, "bank3")
-        weigh(1, 1, 2)
+        weigh(1, 0, 2)
         weave_ds(nc.scalar.copy, 1, 0, 2)
         weigh(1, 2, J)
         weave_ds(nc.scalar.copy, 1, 2, J)
         nc.vector.quantize_mx(out=qm_codes[:].bitcast(E4M3X4), scales=qm_scales[:], in_=qm_cols[:])
         keys_gradient(0)
         place(nc.scalar.copy, 0)
-        quantise_v(3 * C, N, v_last)
+        quantise_v(3 * C, N, v_last[:])
         scores_gradient(3, 0, 2, "bank0")
         scores_gradient(3, 2, J, "bank1")
         weigh(2, 0, J)

@@ -203,9 +203,9 @@ def tile_attend_bwd_kernel(tc, doT, vT, p, delta, qm, offs, out):
             )
             dk[c] = bank
 
-        def place(engine_copy, c):
+        def place(engine_copy, c, engine_scatter=scalar_cast):
             engine_copy(dk_cols[c][:], dk[c][:])
-            nc.scalar.activation(window[:].indirect(listed(c * C, (c + 1) * C)), dk_cols[c][:], ACT.Copy)
+            engine_scatter(window[:].indirect(listed(c * C, (c + 1) * C)), dk_cols[c][:])
 
         for t in range(J):
             scores_gradient(0, t, t + 1, f"bank{t}")
@@ -236,6 +236,6 @@ def tile_attend_bwd_kernel(tc, doT, vT, p, delta, qm, offs, out):
         keys_gradient(2)
         weave_ds(nc.vector.tensor_copy, 3, 0, J)
         keys_gradient(3)
-        place(nc.scalar.copy, 2)
-        place(nc.vector.tensor_copy, 3)
+        place(nc.vector.tensor_copy, 2)
+        place(nc.vector.tensor_copy, 3, nc.vector.tensor_copy)
         nc.sync.dma_start(out=out, in_=window[:])

@@ -28,7 +28,7 @@ NV = 256
 P_FIRST = 2 * J * QH
 DO_SECOND = P_FIRST + 4 * J * C
 MH = QH // J
-TAGS = ("ds_a", "ds_b", "ds_b", "ds_d")
+DS_FIRST = DO_SECOND + 4 * J * QH
 
 
 def tile_attend_bwd_kernel(tc, doT, vT, p, delta, qm, offs, out):
@@ -50,9 +50,14 @@ def tile_attend_bwd_kernel(tc, doT, vT, p, delta, qm, offs, out):
         def scalar_cast(dst, src):
             nc.scalar.activation(dst, src, ACT.Copy)
 
-        def pool_weave(dst, src):
+        def pool_weave(dst, src, j0, j1):
             nc.gpsimd.tensor_scalar(
-                dst.rearrange("p (s j) -> p s j", j=J), src.rearrange("p j s -> p s j"), 1.0, 0.0, ALU.mult, ALU.add
+                dst.rearrange("p (s j) -> p s j", j=J)[:, :, j0:j1],
+                src.rearrange("p j s -> p s j")[:, :, j0:j1],
+                1.0,
+                0.0,
+                ALU.mult,
+                ALU.add,
             )
 
         offsets = keep.tile([P, N // 16], U16, name="offsets")
@@ -74,7 +79,7 @@ def tile_attend_bwd_kernel(tc, doT, vT, p, delta, qm, offs, out):
         nc.sync.dma_start(out=delta_col[:], in_=delta[0].rearrange("(p j) o -> p (j o)", j=J))
         p_rows = p[0].rearrange("(p j) s -> p j s", j=J)
         p_raw = []
-        for s0, s1 in ((0, C), (C, 2 * C), (2 * C, N)):
+        for s0, s1 in ((0, C), (C, 2 * C), (2 * C, 3 * C), (3 * C, N)):
             if s0 == 0:
                 t = reused.tile([P, J, C], F32, name="p_first", align_bytes=64, offset=P_FIRST)
             else:
@@ -171,24 +176,31 @@ def tile_attend_bwd_kernel(tc, doT, vT, p, delta, qm, offs, out):
                 dp[c, t] = bank[:, t - t0, :]
                 dp_pass(dp[c, t], c, t)
 
-        ds_rows = [keep.tile([P, J, C], BF16, name=f"ds_rows{c}") for c in range(J)]
+        ds_rows = {}
         ds_cols = {}
         dk_cols = [keep.tile([P, C], F32, name=f"dk_cols{c}") for c in range(J)]
         dk = {}
 
         def weigh(c, t0, t1):
+            if t0 == 0:
+                ds_rows[c] = keep.tile([P, J, C], BF16, name=f"ds_rows{c}", tag=f"rows{c % 2}")
             for t in range(t0, t1):
                 nc.vector.scalar_tensor_tensor(
                     ds_rows[c][:, t, :], dp[c, t], delta_col[:, t : t + 1], p_raw[c][:, t, :], ALU.subtract, ALU.mult
                 )
 
         def weave_ds(engine_copy, c, j0, j1):
-            if j0 == 0:
-                ds_cols[c] = keep.tile([P, J * C], BF16, name=f"ds_cols{c}", tag=TAGS[c], align_bytes=64)
+            if j0 == 0 and c == 2:
+                ds_cols[c] = reused.tile([P, J * C], BF16, name=f"ds_cols{c}", align_bytes=64, offset=DS_FIRST)
+            elif j0 == 0:
+                ds_cols[c] = keep.tile([P, J * C], BF16, name=f"ds_cols{c}", align_bytes=64)
             weave(engine_copy, ds_cols[c][:], ds_rows[c], j0, j1)
 
         def keys_gradient(c):
-            codes = keep.tile([P, C], U32, name=f"ds_codes{c}", align_bytes=64)
+            if c == 0:
+                codes = reused.tile([P, C], U32, name=f"ds_codes{c}", align_bytes=64, offset=DS_FIRST)
+            else:
+                codes = keep.tile([P, C], U32, name=f"ds_codes{c}", align_bytes=64)
             scales = keep.tile([P, C], U8, name=f"ds_scales{c}", align_bytes=64)
             nc.vector.quantize_mx(out=codes[:].bitcast(E5M2X4), scales=scales[:], in_=ds_cols[c][:])
             bank = psum.tile([P, C], F32, name=f"dk{c}", tag=("bank7", "bank2", "bank4", "bank5")[c])
@@ -223,14 +235,16 @@ def tile_attend_bwd_kernel(tc, doT, vT, p, delta, qm, offs, out):
         weave_ds(nc.scalar.copy, 1, 2, J)
         nc.vector.quantize_mx(out=qm_codes[:].bitcast(E4M3X4), scales=qm_scales[:], in_=qm_cols[:])
         keys_gradient(0)
-        place(nc.scalar.copy, 0)
+        nc.scalar.copy(dk_cols[0][:], dk[0][:])
         quantise_v(3 * C, N, v_last[:])
         scores_gradient(3, 0, 2, "bank0")
         scores_gradient(3, 2, J, "bank1")
-        weigh(2, 0, J)
+        weigh(2, 0, 2)
+        weave_ds(nc.scalar.copy, 2, 0, 2)
+        scalar_cast(window[:].indirect(listed(0, C)), dk_cols[0][:])
+        weigh(2, 2, J)
         keys_gradient(1)
-        ds_cols[2] = keep.tile([P, J * C], BF16, name="ds_cols2", tag=TAGS[2], align_bytes=64)
-        pool_weave(ds_cols[2][:], ds_rows[2][:])
+        pool_weave(ds_cols[2][:], ds_rows[2][:], 2, J)
         place(nc.scalar.copy, 1)
         weigh(3, 0, J)
         keys_gradient(2)

from contextlib import ExitStack

import concourse.mybir as mybir

FLOPS = 335544320

F32 = mybir.dt.float32
BF16 = mybir.dt.bfloat16
U32 = mybir.dt.uint32
U16 = mybir.dt.uint16
U8 = mybir.dt.uint8
E4M3X4 = mybir.dt.float8_e4m3fn_x4
E5M2X4 = mybir.dt.float8_e5m2_x4
ALU = mybir.AluOpType
ACT = mybir.ActivationFunctionType

P = 128
J = 4
Q = 512
N = 512
T = 1024
D = 128
C = 128
QH = Q // 2
WEAVE_OUT = "p (c i j) -> p c j i"
WEAVE_IN = "p j (c i) -> p c j i"
NV = 256
P_FIRST = 2 * J * QH
DO_SECOND = P_FIRST + 4 * J * C
MH = QH // J
DS_FIRST = DO_SECOND + 4 * J * QH


def tile_attend_bwd_kernel(tc, doT, vT, p, delta, qm, offs, out):
    nc = tc.nc
    with ExitStack() as ctx:
        keep = ctx.enter_context(tc.tile_pool(name="keep", bufs=1))
        reused = ctx.enter_context(tc.tile_pool(name="reused", bufs=1))
        psum = ctx.enter_context(tc.psum_pool(name="psum", bufs=1))

        def listed(s0, s1):
            return offsets[:, s0 // 16 : s1 // 16]

        def weave(engine_copy, dst, src, j0, j1):
            engine_copy(
                dst.rearrange(WEAVE_OUT, i=4, j=J)[:, :, j0:j1, :],
                src[:, j0:j1, :].rearrange(WEAVE_IN, i=4),
            )

        def scalar_cast(dst, src):
            nc.scalar.activation(dst, src, ACT.Copy)

        def pool_weave(dst, src, j0, j1):
            nc.gpsimd.tensor_scalar(
                dst.rearrange("p (s j) -> p s j", j=J)[:, :, j0:j1],
                src.rearrange("p j s -> p s j")[:, :, j0:j1],
                1.0,
                0.0,
                ALU.mult,
                ALU.add,
            )

        offsets = keep.tile([P, N // 16], U16, name="offsets")
        do_rows = doT[0].rearrange("(p j) q -> p j q", j=J)
        v_rows = vT.rearrange("(p j) t -> p j t", j=J)
        do_raw = [
            keep.tile([P, J, QH], F32, name="do_first"),
            reused.tile([P, J, QH], F32, name="do_second", align_bytes=64, offset=DO_SECOND),
        ]
        v_raw = [keep.tile([P, T], F32, name=f"v_raw{j}") for j in range(J)]
        nc.sync.dma_start(out=do_raw[0][:], in_=do_rows[:, :, 0:QH])
        nc.sync.dma_start(offsets[:], offs)
        for j in range(J):
            nc.sync.dma_start(out=v_raw[j][:], in_=v_rows[:, j, :])
        nc.sync.dma_start(out=do_raw[1][:], in_=do_rows[:, :, QH:Q])
        qm_raw = keep.tile([P, J, D], F32, name="qm_raw")
        nc.sync.dma_start(out=qm_raw[:], in_=qm[0].rearrange("(p j) d -> p j d", j=J))
        delta_col = keep.tile([P, J], F32, name="delta_col")
        nc.sync.dma_start(out=delta_col[:], in_=delta[0].rearrange("(p j) o -> p (j o)", j=J))
        p_rows = p[0].rearrange("(p j) s -> p j s", j=J)
        p_raw = []
        for s0, s1 in ((0, C), (C, 2 * C), (2 * C, 3 * C), (3 * C, N)):
            if s0 == 0:
                t = reused.tile([P, J, C], F32, name="p_first", align_bytes=64, offset=P_FIRST)
            else:
                t = keep.tile([P, J, s1 - s0], F32, name=f"p_raw{s0}")
            nc.sync.dma_start(out=t[:], in_=p_rows[:, :, s0:s1])
            for c0 in range(0, s1 - s0, C):
                p_raw.append(t[:, :, c0 : c0 + C])

        window = keep.tile([P, T], F32, name="window")
        nc.gpsimd.memset(window[:], 0.0)

        do_cols = [
            keep.tile([P, J * QH], BF16, name="do_cols_low", align_bytes=64),
            reused.tile([P, J * QH], BF16, name="do_cols_high", align_bytes=64, offset=0),
        ]
        do_codes = keep.tile([P, Q], U32, name="do_codes", align_bytes=64)
        do_scales = keep.tile([P, Q], U8, name="do_scales", align_bytes=64)

        def weave_do(engine_copy, h, t0, t1, m0=0, m1=MH):
            engine_copy(
                do_cols[t0 // 2][:].rearrange("p (t h m j) -> p h m j t", t=2, h=2, j=J)[:, h, m0:m1, :, :],
                do_raw[h][:].rearrange("p j (m t) -> p m j t", t=J)[:, m0:m1, :, t0:t1],
            )

        def quantise_do(h, t0, t1):
            for t in range(t0, t1):
                c0 = t * P + h * (P // 2)
                cols = slice(c0, c0 + P // 2)
                nc.vector.quantize_mx(
                    out=do_codes[:, cols].bitcast(E5M2X4),
                    scales=do_scales[:, cols],
                    in_=do_cols[t // 2][:, J * (c0 % QH) : J * (c0 % QH + P // 2)],
                )

        v_low = keep.tile([P, J * NV], BF16, name="v_low", align_bytes=64)
        v_lanes = v_low[:].rearrange("p (s j) -> p s j", j=J)
        v_picked = keep.tile([P, J, N - NV], BF16, name="v_picked")
        v_codes = {}
        v_scales = keep.tile([P, N], U8, name="v_scales", align_bytes=64)

        def quantise_v(s0, s1, src):
            if s0 == C:
                codes = reused.tile([P, C], U32, name=f"v_codes{s0}", align_bytes=64, offset=0)
            elif s0 == 2 * C:
                codes = reused.tile([P, C], U32, name=f"v_codes{s0}", align_bytes=64, offset=DO_SECOND)
            else:
                codes = keep.tile([P, C], U32, name=f"v_codes{s0}", align_bytes=64)
            v_codes[s0 // C] = codes
            nc.vector.quantize_mx(out=codes[:].bitcast(E4M3X4), scales=v_scales[:, s0:s1], in_=src)

        weave_do(nc.vector.tensor_copy, 0, 0, 2)
        weave_do(scalar_cast, 0, 2, J)
        quantise_do(0, 0, J)
        for j in range(J):
            for s0, s1 in ((NV, N),) if j < J - 1 else ((NV, NV + C), (NV + C, N)):
                nc.scalar.activation(v_picked[:, j, s0 - NV : s1 - NV], v_raw[j][:].indirect(listed(s0, s1)), ACT.Copy)
            for s0, s1 in ((0, NV),) if j < J - 1 else ((0, C), (C, NV)):
                nc.vector.tensor_copy(v_lanes[:, s0:s1, j], v_raw[j][:].indirect(listed(s0, s1)))
        v_third = keep.tile([P, J * C], BF16, name="v_third", align_bytes=64)
        weave(nc.scalar.copy, v_third[:], v_picked[:, :, 0:C], 0, J)
        quantise_v(0, C, v_low[:, 0 : J * C])
        weave_do(nc.vector.tensor_copy, 1, 0, 2)
        weave_do(nc.vector.tensor_copy, 1, 2, J, 0, MH // 2)
        weave_do(nc.scalar.copy, 1, 2, J, MH // 2, MH)
        quantise_do(1, 0, J)
        quantise_v(C, NV, v_low[:, J * C : J * NV])
        quantise_v(NV, NV + C, v_third[:])

        qm_cols = keep.tile([P, J * D], BF16, name="qm_cols", align_bytes=64)
        qm_scales = keep.tile([P, D], U8, name="qm_scales", align_bytes=64)
        weave(nc.scalar.copy, qm_cols[:], qm_raw, 0, J)
        v_last = reused.tile([P, J * C], BF16, name="v_last", align_bytes=64, offset=DO_SECOND + 4 * C)
        weave(nc.scalar.copy, v_last[:], v_picked[:, :, C : 2 * C], 0, J)
        qm_codes = reused.tile([P, D], U32, name="qm_codes", align_bytes=64, offset=P_FIRST)

        def dp_pass(dst, c, t):
            cols = slice(t * P, (t + 1) * P)
            slots = slice(c * C, (c + 1) * C)
            nc.tensor.matmul_mx(
                out=dst,
                lhsT=do_codes[:, cols].bitcast(E5M2X4),
                lhsT_scale=do_scales[:, cols],
                rhs=v_codes[c][:].bitcast(E4M3X4),
                rhs_scale=v_scales[:, slots],
                start=True,
                stop=True,
            )

        dp = {}

        def scores_gradient(c, t0, t1, bank_name):
            bank = psum.tile([P, t1 - t0, C], F32, name=f"dp{c}_{t0}", tag=bank_name)
            for t in range(t0, t1):
                dp[c, t] = bank[:, t - t0, :]
                dp_pass(dp[c, t], c, t)

        ds_rows = {}
        ds_cols = {}
        dk_cols = [keep.tile([P, C], F32, name=f"dk_cols{c}") for c in range(J)]
        dk = {}

        def weigh(c, t0, t1):
            if t0 == 0:
                ds_rows[c] = keep.tile([P, J, C], BF16, name=f"ds_rows{c}", tag=f"rows{c % 2}")
            for t in range(t0, t1):
                nc.vector.scalar_tensor_tensor(
                    ds_rows[c][:, t, :], dp[c, t], delta_col[:, t : t + 1], p_raw[c][:, t, :], ALU.subtract, ALU.mult
                )

        def weave_ds(engine_copy, c, j0, j1):
            if j0 == 0 and c == 2:
                ds_cols[c] = reused.tile([P, J * C], BF16, name=f"ds_cols{c}", align_bytes=64, offset=DS_FIRST)
            elif j0 == 0:
                ds_cols[c] = keep.tile([P, J * C], BF16, name=f"ds_cols{c}", align_bytes=64)
            weave(engine_copy, ds_cols[c][:], ds_rows[c], j0, j1)

        def keys_gradient(c):
            if c == 0:
                codes = reused.tile([P, C], U32, name=f"ds_codes{c}", align_bytes=64, offset=DS_FIRST)
            else:
                codes = keep.tile([P, C], U32, name=f"ds_codes{c}", align_bytes=64)
            scales = keep.tile([P, C], U8, name=f"ds_scales{c}", align_bytes=64)
            nc.vector.quantize_mx(out=codes[:].bitcast(E5M2X4), scales=scales[:], in_=ds_cols[c][:])
            bank = psum.tile([P, C], F32, name=f"dk{c}", tag=("bank7", "bank2", "bank4", "bank5")[c])
            nc.tensor.matmul_mx(
                out=bank[:],
                lhsT=qm_codes[:].bitcast(E4M3X4),
                lhsT_scale=qm_scales[:],
                rhs=codes[:].bitcast(E5M2X4),
                rhs_scale=scales[:],
                start=True,
                stop=True,
            )
            dk[c] = bank

        def place(engine_copy, c, engine_scatter=scalar_cast):
            engine_copy(dk_cols[c][:], dk[c][:])
            engine_scatter(window[:].indirect(listed(c * C, (c + 1) * C)), dk_cols[c][:])

        for t in range(J):
            scores_gradient(0, t, t + 1, f"bank{t}")
        scores_gradient(1, 0, 2, "bank4")
        scores_gradient(1, 2, J, "bank5")
        weigh(0, 0, 2)
        weave_ds(nc.scalar.copy, 0, 0, 2)
        weigh(0, 2, J)
        weave_ds(nc.scalar.copy, 0, 2, J)
        scores_gradient(2, 0, 2, "bank6")
        scores_gradient(2, 2, J, "bank3")
        weigh(1, 0, 2)
        weave_ds(nc.scalar.copy, 1, 0, 2)
        weigh(1, 2, J)
        weave_ds(nc.scalar.copy, 1, 2, J)
        nc.vector.quantize_mx(out=qm_codes[:].bitcast(E4M3X4), scales=qm_scales[:], in_=qm_cols[:])
        keys_gradient(0)
        nc.scalar.copy(dk_cols[0][:], dk[0][:])
        quantise_v(3 * C, N, v_last[:])
        scores_gradient(3, 0, 2, "bank0")
        scores_gradient(3, 2, J, "bank1")
        weigh(2, 0, 2)
        weave_ds(nc.scalar.copy, 2, 0, 2)
        scalar_cast(window[:].indirect(listed(0, C)), dk_cols[0][:])
        weigh(2, 2, J)
        keys_gradient(1)
        pool_weave(ds_cols[2][:], ds_rows[2][:], 2, J)
        place(nc.scalar.copy, 1)
        weigh(3, 0, J)
        keys_gradient(2)
        weave_ds(nc.vector.tensor_copy, 3, 0, J)
        keys_gradient(3)
        place(nc.vector.tensor_copy, 2)
        place(nc.vector.tensor_copy, 3, nc.vector.tensor_copy)
        nc.sync.dma_start(out=out, in_=window[:])
